import numpy as np, ml_dtypes
CORES = [48,51,52,55]
N = 4
BF = ml_dtypes.bfloat16
def gentries(a):
    return np.ascontiguousarray(a.reshape(8, 16, -1).transpose(0, 2, 1)).reshape(8, -1)
def gtable(e):
    e = np.asarray(e); return np.ascontiguousarray(e.reshape(8, -1, 16).transpose(0, 2, 1)).reshape(128, -1).astype(np.int32)
W, H, L, CAP, RO = 2560, 1024, 256, 256, 4
def pick(t, e):
    return np.take_along_axis(t, e[:, None, :], 2)
def at(x, c):
    return pick(x, c.reshape(8, -1)).reshape(8, 16, 16, -1)
def moved(v, dl):
    return np.clip(v + dl[:, :, None, :], 0, 63)
def spot(u):
    return (((u * u) >> 5) + 37 * u) & (H - 1)
def parts(rng):
    x = rng.integers(0, 64, (N, 8, 16, W)); su = rng.integers(0, W, (N, 8, 16, W)); co = np.argsort(rng.random((N, 8, 16, W)), axis=-1)
    dl = rng.integers(-20, 21, (N, 8, 16, L)); la = rng.integers(0, W, (N, 8, L)); lb = rng.integers(0, W, (N, 8, L))
    wt = rng.integers(0, 256, (N, 8, 16)); th = 110 + 20 * np.argsort(rng.random((N, 8)), axis=-1) + rng.integers(0, 20, (N, 8))
    return x, su, co, dl, la, lb, wt, th
def pack(x, su, co, dl, la, lb, wt, th):
    fl = lambda a, n: np.ascontiguousarray(np.asarray(a).reshape(N, 128, n)).astype(np.float32).astype(BF)
    it = lambda a: np.ascontiguousarray(np.asarray(a).reshape(N, 128, W)).astype(np.int32)
    return {"x0": fl(x, W), "su": it(su), "co": it(co), "dl": fl(dl, L), "la": np.stack([gtable(a) for a in la]), "lb": np.stack([gtable(a) for a in lb]),
            "wt": fl(wt, 1), "th": np.asarray(th).reshape(N, 8, 1).astype(np.int32)}
def put(p, c, v):
    w = np.argmax(p == v[..., None], axis=-1); old = p[..., c].copy()
    np.put_along_axis(p, w[..., None], old[..., None], -1); p[..., c] = v
def two(rng, n):
    c = rng.integers(0, 3, (N, 8, 1, n)); return np.where(c < 2, c, rng.integers(0, 2, (N, 8, 16, n)))
def spots(dl, wt):
    return spot(np.sum(63 * wt[:, :, None] * (dl > 0), axis=1) & 4095)
def setup_inputs(rng):
    return pack(*parts(rng))
def setup_inputs_spread(rng):
    x, su, co, dl, la, lb, wt, th = parts(rng)
    p = np.exp2(rng.integers(-2, 3, (N, 8, 1, W))); x = np.minimum((64 * rng.random((N, 8, 16, W)) ** p).astype(np.int64), 63)
    p = np.exp2(rng.integers(-2, 3, (N, 8, 1, W))); su = np.minimum((W * rng.random((N, 8, 16, W)) ** p).astype(np.int64), W - 1)
    dl = np.rint((2 * rng.random((N, 8, 16, L)) - 1) * rng.choice(np.array([0, 1, 3, 9, 27, 63]), (N, 8, 1, L))).astype(np.int64)
    la = np.minimum((W * rng.random((N, 8, L)) ** 2).astype(np.int64), W - 1); lb = W - 1 - np.minimum((W * rng.random((N, 8, L)) ** 2).astype(np.int64), W - 1)
    wt = np.minimum(np.exp2(8 * rng.random((N, 8, 16))).astype(np.int64), 256) - 1
    th = np.where(rng.random((N, 8)) < 0.5, np.minimum(np.exp2(10 * rng.random((N, 8))).astype(np.int64), 1024) - 1, rng.integers(100, 300, (N, 8)))
    return pack(x, su, co, dl, la, lb, wt, th)
def setup_inputs_ends(rng):
    x, su, co, dl, la, lb, wt, th = parts(rng)
    x = 63 * two(rng, W); su = (W - 1) * two(rng, W); dl = 126 * two(rng, L) - 63
    la = (W - 1) * rng.integers(0, 2, (N, 8, L)); lb = (W - 1) * rng.integers(0, 2, (N, 8, L)); la[:, :, L - 1] = W - 1; lb[:, :, 0] = 0
    wt = 255 * rng.integers(0, 2, (N, 8, 16)); wt[:, 0] = 255 * (np.arange(16) & 1); wt[:, 7] = 255
    th = 1023 * rng.integers(0, 2, (N, 8)); th[:, 0] = 1023; th[:, 1] = 0; th[:, 7] = 0; th[0, 6] = 1023
    z = rng.integers(0, 2, (N, 8, 16)); z[:, :, 0] = 1; z[:, :, 15] = 0
    put(co, 0, (W - 1) * z); put(co, W - 1, (W - 1) * (1 - z))
    dl[:, 7] = np.where(rng.random((N, 1, L)) < 0.5, 63, -63); dl[:, 7, :, 0] = 63; dl[:, 7, :, 1] = -63; dl[:, 7, :, L - 1] = 63
    x[:, 7, :, 0] = 0; x[:, 7, :, W - 1] = 0; x[:, 7, :, spot((16 * 63 * 255) & 4095)] = 0
    x[:, 6, :, 0] = 63; x[:, 6, :, W - 1] = 63; dl[:, 6, :, 0] = -63; dl[:, 6, :, L - 1] = -63
    return pack(x, su, co, dl, la, lb, wt, th)
def setup_inputs_corners(rng):
    x, su, co, dl, la, lb, wt, th = parts(rng); th[:] = 0; dl = 126 * rng.integers(0, 2, (N, 8, 16, L)) - 63
    for r in range(N):
        own = spots(dl[r], wt[r]); come = spots(dl[r - 1], wt[r])
        for i in range(8):
            p = np.unique(own[i]); z = p[:0]
            if i % 2: z = p; p = np.setdiff1d(come[i], z)
            n = int(rng.choice(np.array([0, 1, CAP - 1, CAP, CAP + 1, W - H])))
            if r in (0, N - 1): n = (CAP, CAP, CAP + 1, CAP + 1, CAP - 1, CAP - 1, 0, 1)[i]
            if r == 1 and i in (2, 6): n = W - H
            n = min(n, 16 * len(p), W - H)
            a = np.concatenate([z, p]); s = np.stack([rng.permutation(H)[:len(a)] for k in range(16)])
            c = s[:, len(z):].copy().reshape(-1); c[rng.permutation(len(c))[:n]] = H + rng.permutation(W - H)[:n]
            s[:, len(z):] = c.reshape(16, -1)
            rest = np.ones(W, bool); rest[a] = False
            for k in range(16):
                free = np.ones(W, bool); free[s[k]] = False
                co[r, i, k, a] = s[k]; co[r, i, k, rest] = rng.permutation(np.flatnonzero(free))
    return pack(x, su, co, dl, la, lb, wt, th)
def setup_inputs_crowd(rng):
    x, su, co, dl, la, lb, wt, th = parts(rng)
    dl[:, :2] = 126 * rng.integers(0, 2, (N, 2, 16, L)) - 63
    for i in range(8):
        m = (1, 1, 2, 1, 4, 1, 2, 1)[i]; s = rng.integers(0, m, L); z = int(rng.integers(1, L - 1))
        if i % 2: s[z] = m
        la[:, i] = la[:, i][:, s]; lb[:, i] = lb[:, i][:, s]; dl[:, i] = dl[:, i][:, :, s]
    for r in range(N):
        n = spots(dl[r], wt[r])
        put(co[r, 0], int(n[0, 0]), np.full(16, W - 1)); put(co[r, 1], int(n[1, 0]), np.full(16, H))
        if r % 3 < 2: th[r] = 0
        if r % 3 == 0: dl[r, 5, :, L - 1] = 0; lb[r, 5, L - 1] = la[r, 5, L - 1]
        if r % 3 == 1: th[r, 3] = 1; dl[r, 3, :, L - 1] = 0; lb[r, 3, L - 1] = la[r, 3, L - 1]
    return pack(x, su, co, dl, la, lb, wt, th)
def setup_inputs_ties(rng):
    x, su, co, dl, la, lb, wt, th = parts(rng)
    x = 8 * (x >> 4); x[:, 1::2] = 63 - x[:, 1::2]; dl = 8 * rng.integers(-1, 2, (N, 8, 16, L))
    x[:, 3] = 63; x[:, 3, :7] = 62 + np.minimum(rng.integers(0, 4, (N, 7, W)), 1); dl[:, 3] = -63; dl[2, 3, :, 48:] = 0
    put(co[2, 3], 0, H + np.arange(16)); su[2, 3, :, H:H + 16] = H + ((np.arange(16) + 1) & 15)
    su[:, ::2, :, :W // 2] = su[:, ::2, :1, :W // 2].copy()
    la[:, :, 16:32] = la[:, :, :16].copy(); lb[:, :, 16:32] = lb[:, :, :16].copy(); dl[:, :, :, 16:32] = dl[:, :, :, :16].copy()
    lb[:, :, 32:48] = la[:, :, 32:48].copy(); dl[:, :, :, 32:48] = 0
    for r in range(N):
        dd = np.sum(np.abs(at(x[r], pick(co[r], lb[r])) - moved(at(x[r], pick(co[r], la[r])), dl[r])), axis=1)
        th[r] = np.sort(np.min(dd, axis=1), axis=1)[:, L // 2]; th[r, 4:] += rng.integers(0, 2, 4)
        if r == 2: th[r] = 1023; th[r, 3] = np.min(dd[3, :, :32])
    return pack(x, su, co, dl, la, lb, wt, th)
def check_inputs(d):
    bad = []
    for k, lo, hi in (("x0", 0, 63), ("su", 0, W - 1), ("co", 0, W - 1), ("dl", -63, 63), ("la", 0, W - 1), ("lb", 0, W - 1), ("wt", 0, 255), ("th", 0, 1023)):
        a = np.asarray(d[k]).astype(np.float64)
        if not (np.min(a) >= lo and np.max(a) <= hi): bad.append("range of " + k)
        if np.any(a != np.floor(a)): bad.append("whole numbers of " + k)
    if np.any(np.sort(np.asarray(d["co"]), axis=-1) != np.arange(W)): bad.append("a row of co holds every node once")
    return bad
def reference(x0, su, co, dl, la, lb, wt, th):
    x = x0.astype(np.float32).astype(np.int32).reshape(N, 8, 16, W); s = su.astype(np.int64).reshape(N, 8, 16, W); c = co.astype(np.int64).reshape(N, 8, 16, W)
    sh = dl.astype(np.float32).astype(np.int32).reshape(N, 8, 16, L); w = wt.astype(np.float32).astype(np.int32).reshape(N, 8, 16, 1, 1); lim = th.astype(np.int64).reshape(N, 8, 1)
    a = np.stack([gentries(v) for v in la]).astype(np.int64); b = np.stack([gentries(v) for v in lb]).astype(np.int64)
    flag = np.zeros((N, 8, W), bool); last = np.zeros(N, np.int64)
    for t in range(RO):
        for r in range(N):
            q = (r - t) % N
            d = pick(c[r], a[q]); f = pick(c[r], b[q])
            dist = np.sum(np.abs(at(x[r], f) - moved(at(x[r], d), sh[q])), axis=1)
            k = np.argmin(dist, axis=1)[:, None, :]
            dk = np.take_along_axis(d, k, 1)[:, 0]; fk = np.take_along_axis(f, k, 1)[:, 0]
            same = np.take_along_axis(dist, k, 1)[:, 0] < lim[r] + (last[r] & 63)
            e = moved(at(x[r], pick(s[r], dk)), sh[q])
            n = spot(np.sum(w[r] * e, axis=1).astype(np.int64) & 4095)
            j = np.argmax(np.sum(np.abs(at(x[r], n) - e), axis=1), axis=1)[:, None, :]
            nj = np.take_along_axis(n, j, 1)[:, 0]; ej = np.take_along_axis(e, j[:, None], 2)[:, :, 0]
            for i in range(8):
                lane = np.flatnonzero(~same[i]); place, first = np.unique(nj[i, lane], return_index=True)
                x[r, i][:, place] = ej[i][:, lane[first]]
                flag[r, i, c[r, i][:, place].reshape(-1)] = True; flag[r, i, :H] = False
                v = np.flatnonzero(flag[r, i])[:CAP]
                z = x[r, i][:, s[r, i][:, v]]
                x[r, i][:, v] = (np.max(z, axis=1) + np.min(z, axis=1)) >> 1
                flag[r, i, v] = False
            last[r] = np.sum(~same)
            a[q] = np.where(same, dk, a[q]); b[q] = np.where(same, fk, b[q])
    return {"yx": x.reshape(N, 128, W).astype(np.float32).astype(BF), "ya": np.stack([gtable(a[(r - RO + 1) % N]) for r in range(N)]).astype(np.float32),
            "yb": np.stack([gtable(b[(r - RO + 1) % N]) for r in range(N)]).astype(np.float32)}

@@ -1,0 +1,473 @@
+from concourse.mybir import AluOpType as OP, AxisListType, ActivationFunctionType as AF
+
+R = 4
+SCRATCH = {}
+for _n, _w, _t in [
+        ("Xw", 2816, "bfloat16"), ("coI", 2688, "int32"), ("coH", 2560, "bfloat16"), ("coL", 2560, "bfloat16"), ("tmpI", 2560, "int32"),
+        ("suI", 2816, "int32"), ("sh0", 4096, "bfloat16"), ("sh1", 4096, "bfloat16"), ("dls", 1024, "bfloat16"),
+        ("M", 4096, "bfloat16"), ("E", 4096, "bfloat16"), ("z", 4096, "bfloat16"), ("az", 4096, "bfloat16"), ("gF", 4096, "bfloat16"),
+        ("Fv", 2688, "bfloat16"), ("Fs0", 2688, "float32"), ("Fs1", 2688, "float32"), ("FsB0", 1536, "bfloat16"), ("FsB1", 1536, "bfloat16"),
+        ("Vw0", 1792, "float32"), ("Vw1", 1792, "float32"), ("iotaV", 1536, "float32"),
+        ("ident", 128, "bfloat16"), ("nident", 128, "bfloat16"), ("identF", 128, "float32"), ("grp", 128, "bfloat16"), ("grpF", 128, "float32"),
+        ("onesF", 128, "float32"), ("onesB", 128, "bfloat16"), ("ntri", 128, "bfloat16"), ("selX", 2048, "bfloat16"), ("WT", 2048, "bfloat16"),
+        ("g8", 8, "float32"), ("g8s", 24, "float32"), ("g8p", 48, "bfloat16"), ("cK", 640, "bfloat16"),
+        ("jm", 1024, "float32"), ("segN", 512, "float32"), ("segX", 128, "float32"), ("seg1", 256, "float32"), ("rN", 512, "bfloat16"), ("rX", 512, "bfloat16"),
+        ("dm", 640, "float32"), ("ltm", 128, "bfloat16"), ("pI", 8, "int32"), ("pT", 32, "int32"), ("pF", 8, "float32"),
+        ("eI", 64, "int32"), ("LE", 40, "uint16"), ("LX", 8, "uint16"), ("LP", 8, "uint16"), ("Ld", 96, "float32"), ("Ld1", 96, "float32"),
+        ("idx", 8, "float32"), ("EB", 8, "float32"), ("one96", 96, "bfloat16"),
+        ("stv", 512, "bfloat16"), ("sts", 512, "float32"), ("wt_", 8, "bfloat16"), ("wtF", 8, "float32"), ("thI", 8, "int32"), ("thF", 8, "float32"),
+        ("thr", 8, "float32"), ("th16", 8, "float32"), ("gT", 128, "float32"), ("laI", 16, "int32"), ("lbI", 16, "int32"),
+        ("abI", 32, "float32"), ("land", 128, "float32"), ("abo", 128, "float32"), ("abU", 32, "uint16"),
+        ("al", 16, "float32"), ("acc", 8, "float32"), ("acJ", 16, "int32"), ("accI", 16, "int32"),
+        ("df", 512, "uint16"), ("dfH", 512, "bfloat16"), ("dfL", 512, "bfloat16"),
+        ("Fp", 96, "bfloat16"), ("Fn", 96, "bfloat16"), ("Fi", 96, "bfloat16"), ("t96", 96, "float32"), ("s96", 96, "float32"), ("Lv", 96, "uint16"),
+        ("vX", 256, "float32"), ("vS", 256, "float32"), ("vL", 16, "uint16"), ("sR", 256, "uint16"), ("rs", 256, "float32"), ("rI", 256, "int32")]:
+    SCRATCH[_n] = ("sbuf", [128, _w], _t)
+HALF = {}
+for _n, _w, _t in [("S", 640, "float32"), ("B", 640, "float32"), ("dL", 8, "uint16"), ("ta", 16, "float32"), ("sT", 128, "uint16"),
+                   ("uI", 128, "int32"), ("uA", 128, "int32"), ("uL", 128, "float32"), ("nO", 128, "uint16"), ("nP", 128, "float32"),
+                   ("vI", 8, "int32"), ("nI", 8, "int32"), ("jI", 8, "int32"), ("eO", 8, "uint16"), ("nS", 8, "float32"), ("nt", 8, "float32"), ("nl", 8, "float32"),
+                   ("nBs", 128, "float32"), ("EQ", 1024, "bfloat16"), ("oU", 8, "uint16"), ("oD", 16, "uint16"), ("T1", 256, "float32"),
+                   ("T2", 256, "float32"), ("fL", 128, "uint16"), ("eS", 128, "bfloat16")]:
+    SCRATCH[_n] = ("sbuf", [128, 2 * _w], _t)
+    HALF[_n] = _w
+for _b in range(8):
+    SCRATCH["P%d" % _b] = ("psum", [128, 512], "float32")
+
+LOADS = ["la", "lb", "dl", "co0", "co1", "x0", "x1", "su0", "su1", "wt", "th"]
+SEMAPHORES = ["sv", "ss", "sp", "sg", "ls", "so"] + ["ld_" + n for n in LOADS] + ["rdl%d" % t for t in (1, 2, 3)] + ["rab%d" % t for t in (1, 2, 3)]
+
+CY, WAKE, LAM, GA, SC = 0.83e-3, 0.1, 0.02, 1.5, 3.5
+SPATH = {1: ((1, 3), (1, 3)), 2: ((1, 3), (1, 3))}
+MPATH = {1: ((1, 3), (3,)), 2: ((3,), (3,))}
+FLAG_S = (tuple(range(12)), tuple(range(6)))
+REN_S = (1, 2, 3, 4, 5, 6, 7)
+ORDER = {}
+
+
+def schedule(ops):
+    n = len(ops)
+    succ = [[] for _ in ops]
+    for i, o in enumerate(ops):
+        for d in o["deps"]:
+            succ[d].append(i)
+    pri = [0.0] * n
+    for i in range(n - 1, -1, -1):
+        pri[i] = ops[i]["c"] + max([pri[s] + WAKE for s in succ[i]], default=0.0)
+    need = [len(o["deps"]) for o in ops]
+    early, start, free, out = [0.0] * n, [0.0] * n, {}, []
+    ready = {i for i in range(n) if need[i] == 0}
+    while ready:
+        best = {}
+        for i in ready:
+            e = ops[i]["e"]
+            best[e] = min(best.get(e, 1e18), max(early[i], free.get(e, 0.0)))
+        e = min(best, key=lambda q: (best[q], q))
+        i = max((j for j in ready if ops[j]["e"] == e and max(early[j], free.get(e, 0.0)) <= best[e] + 0.02), key=lambda j: (pri[j] - LAM * j, -j))
+        s = start[i] = max(early[i], free.get(e, 0.0))
+        free[e] = s + (0.05 if ops[i]["async"] else ops[i]["c"])
+        ready.discard(i)
+        out.append(i)
+        for j in succ[i]:
+            early[j] = max(early[j], s + ops[i]["c"] + WAKE)
+            need[j] -= 1
+            if need[j] == 0:
+                ready.add(j)
+    return out, start, max(start[i] + ops[i]["c"] for i in range(n))
+
+
+def rank_program(g, core, T, topo):
+    rank = T.rank_of(core)
+    if rank is None:
+        return
+    N = len(T.cores)
+    V, S, PE = g.vector, g.scalar, g.tensor
+    ops, lastw, readers = [], {}, {}
+
+    def op(e, c, r, w, fs, sem=None, val=None, isasync=False, order=()):
+        i = len(ops)
+        deps, soft = {lastw[t] for t in r if t in lastw}, set(order)
+        for t in w:
+            if t in lastw:
+                (soft if t[0] == "P" and ops[lastw[t]]["e"] == e else deps).add(lastw[t])
+            deps.update(readers.get(t, ()))
+        for t in r:
+            readers.setdefault(t, []).append(i)
+        for t in w:
+            lastw[t] = i
+            readers[t] = []
+        deps.discard(i)
+        ops.append({"e": e, "c": c, "hard": sorted(deps), "deps": sorted(deps | soft), "f": fs, "sem": sem, "val": val, "async": isasync})
+        return i
+
+    esem = {"V": "sv", "S": "ss", "PE": "sp", "G": "sg"}
+    vop = lambda n, r, w, f, cy=1.0: op("V", 0.055 + max(n * cy, 64) * CY, r, w, [f])
+    sop = lambda n, r, w, f, cy=1.0: op("S", 0.07 + max(n * cy, 64) * CY, r, w, [f])
+    vg = lambda n, r, w, f: vop(n, r, w, f, GA)
+    sg = lambda n, r, w, f: sop(n, r, w, f, GA)
+    pop = lambda cyc, r, w, fs: op("PE", cyc * CY, r, w, fs)
+    gop = lambda n, r, w, f: op("G", 0.17 + 2 * n * CY, r, w, [f])
+    load = lambda q, name, c, w, out, in_: op(q, c, [], w, [lambda: (g.sync if q == "Y" else S).dma_start(out, in_)], "ld_" + name, 16, True)
+
+    def ts(out, a, s1, s2, o0, o1=None):
+        return (lambda: V.tensor_scalar(out, a, s1, s2, o0)) if o1 is None else (lambda: V.tensor_scalar(out, a, s1, s2, o0, o1))
+
+    tt = lambda out, a, b, o: (lambda: V.tensor_tensor(out, a, b, o))
+    cp = lambda out, a: (lambda: V.tensor_copy(out, a))
+    fill = lambda out, c: (lambda: V.memset(out, c))
+    act = lambda out, a, f, **k: (lambda: S.activation(out, a, f, **k))
+    mm = lambda out, l, r, a, b: (lambda: PE.matmul(out, l, r, a, b))
+    scan = lambda out, a, b, i, o0, o1: (lambda: V.tensor_tensor_scan(out, a, b, i, o0, o1))
+    iof = lambda out, pat, base: (lambda: g.iota(out, pat, base, 0, allow_small_or_imprecise_dtypes=True))
+    ioi = lambda out, pat, base, cm: (lambda: g.iota(out, pat, base, cm))
+    sel = lambda out, a, pat, o, base, cm: (lambda: g.affine_select(out, a, pat, o, 0.0, base, cm))
+    turn = [0]
+
+    def bank():
+        turn[0] += 1
+        return 5 + turn[0] % 3
+
+    load("Y", "la", 2, ["laI"], T.laI[:], T.la[:])
+    load("Y", "lb", 2, ["lbI"], T.lbI[:], T.lb[:])
+    load("S", "dl", 2.5, ["dl0"], T.dls[:, 0:256], T.dl[:])
+    load("Y", "co0", 6, ["co0"], T.coI[:, 0:1280], T.co[:, 0:1280])
+    load("S", "co1", 6, ["co1"], T.coI[:, 1280:2560], T.co[:, 1280:2560])
+    load("Y", "x0", 8, ["X", "Xa"], T.Xw[:, 0:1280], T.x0[:, 0:1280])
+    load("S", "x1", 8, ["Xb"], T.Xw[:, 1280:2560], T.x0[:, 1280:2560])
+    load("Y", "wt", 3, ["wt"], T.wt_[:, 0:1], T.wt[:])
+    load("Y", "th", 3, ["thI"], T.thI[0:8, 0:1], T.th[:])
+    load("Y", "su0", 12, ["su0"], T.suI[:, 0:1280], T.su[:, 0:1280])
+    load("Y", "su1", 12, ["su1"], T.suI[:, 1280:2560], T.su[:, 1280:2560])
+    co_t, su_t, x_t = ["co0", "co1", "co2"], ["su0", "su1", "su2"], ["X", "Xa", "Xb"]
+
+    gop(1, [], ["pI"], ioi(T.pI[:, 0:1], [[0, 1]], 0, 1))
+    gop(256, [], ["jm"], iof(T.jm[:], [[0, 64], [1, 16]], 0))
+    vop(1, ["pI"], ["pT"], ts(T.pT[:, 0:1], T.pI[:, 0:1], 15, None, OP.bitwise_and))
+    vop(1, ["pT"], ["pF"], cp(T.pF[:, 0:1], T.pT[:, 0:1]))
+    vop(640, ["jm", "pF"], ["dm"], ts(T.dm[:], T.jm[:, 0:640], T.pF[:, 0:1], None, OP.is_equal))
+    vop(512, ["jm"], ["segN"], ts(T.segN[:], T.jm[:, 0:512], 0.0, 1e9, OP.is_equal, OP.mult))
+    gop(40, [], ["eI"], ioi(T.eI[:, 0:40], [[16, 40]], 15, 0))
+    vop(40, ["eI"], ["LE"], cp(T.LE[:], T.eI[:, 0:40]))
+    vop(128, [], ["onesB"], fill(T.onesB[:], 1.0))
+    vop(128, [], ["onesF"], fill(T.onesF[:], 1.0))
+    gop(128, ["onesB"], ["ident"], sel(T.ident[:], T.onesB[:], [[-1, 128]], OP.is_equal, 0, 1))
+    vop(128, ["ident"], ["nident"], ts(T.nident[:], T.ident[:], -1.0, None, OP.mult))
+    gop(8, ["onesF"], ["g8"], sel(T.g8[:], T.onesF[:, 0:8], [[-16, 8]], OP.is_ge, 0, 1))
+    gop(8, ["g8"], ["g8"], sel(T.g8[:], T.g8[:], [[16, 8]], OP.is_ge, 15, -1))
+    for i, s in enumerate((2048.0, 512.0, 2048.0, 512.0, 16.0, 16384.0)):
+        vop(8, ["g8"], ["g8p"], ts(T.g8p[:, 8 * i:8 * i + 8], T.g8[:], s, None, OP.mult))
+    for i, s in enumerate((32.0, -4128.0, 1.0)):
+        vop(8, ["g8"], ["g8s"], ts(T.g8s[:, 8 * i:8 * i + 8], T.g8[:], s, None, OP.mult))
+    for i, s in enumerate((128, 32, 128, 32, 1)):
+        gop(128, [], ["cK"], iof(T.cK[:, 128 * i:128 * i + 128], [[0, 8], [s, 16]], 0))
+    gop(128, ["onesF"], ["grpF"], sel(T.grpF[:], T.onesF[:], [[-16, 8], [0, 16]], OP.is_ge, 0, 1))
+    gop(128, ["grpF"], ["grpF"], sel(T.grpF[:], T.grpF[:], [[16, 8], [0, 16]], OP.is_ge, 15, -1))
+    vop(128, ["grpF"], ["grp"], cp(T.grp[:], T.grpF[:]))
+    gop(128, ["onesF"], ["gT"], sel(T.gT[:], T.onesF[:], [[1, 8], [0, 16]], OP.is_equal, 0, -1))
+    gop(128, ["onesF"], ["identF"], sel(T.identF[:], T.onesF[:], [[-1, 128]], OP.is_equal, 0, 1))
+    vop(1, ["thI"], ["thF"], cp(T.thF[0:8, 0:1], T.thI[0:8, 0:1]))
+    pop(256, ["gT", "thF"], ["P7"], [mm(T.P7[:, 0:1], T.gT[0:8, :], T.thF[0:8, 0:1], True, True)])
+    vop(1, [], ["th16", "P7"], ts(T.th16[:, 0:1], T.P7[:, 0:1], 16.0, None, OP.mult))
+    vop(1, ["th16"], ["thr"], cp(T.thr[:, 0:1], T.th16[:, 0:1]))
+    for j in range(16):
+        gop(128, ["grp"], ["selX"], sel(T.selX[:, 128 * j:128 * j + 128], T.grp[:], [[0, 8], [1, 16]], OP.is_equal, -j, 0))
+    vop(1, ["wt"], ["wtF"], cp(T.wtF[:, 0:1], T.wt_[:, 0:1]))
+    vop(2048, ["selX", "wtF"], ["WT"], ts(T.WT[:], T.selX[:], T.wtF[:, 0:1], None, OP.mult), 0.5)
+    vop(128, ["jm"], ["segX"], ts(T.segX[:], T.jm[:, 0:128], 0.0, 1e9, OP.is_gt, OP.mult))
+    vop(256, ["jm"], ["seg1"], ts(T.seg1[:], T.jm[:, 0:256], 0.0, None, OP.is_gt))
+    vop(512, ["jm"], ["rN"], ts(T.rN[:], T.jm[:, 0:512], 0.0, 64.0, OP.is_equal, OP.mult))
+    vop(512, ["jm"], ["rX"], ts(T.rX[:], T.jm[:, 0:512], 0.0, 64.0, OP.is_gt, OP.mult))
+    vop(128, ["jm", "pF"], ["ltm"], ts(T.ltm[:], T.jm[:, 0:128], T.pF[:, 0:1], None, OP.is_gt))
+    vop(96, [], ["one96"], fill(T.one96[:], 1.0))
+    vop(96, [], ["Fp"], fill(T.Fp[:], 0.0))
+    vop(2688, [], ["Fv"], fill(T.Fv[:], 0.0), 0.5)
+    for h in (0, 1):
+        gop(2688, [], ["Fs%d" % h], iof(T["Fs%d" % h][:], [[0, 2688]], 0))
+    vop(256, [], ["su2"], fill(T.suI[:, 2560:2816], 0))
+    gop(128, [], ["co2"], ioi(T.coI[:, 2560:2688], [[1, 128]], 2560, 0))
+    gop(1536, [], ["iotaV"], iof(T.iotaV[:], [[1, 1536]], 1024))
+    gop(8, [], ["eI2"], ioi(T.eI[:, 48:56], [[1, 8]], 0, 0))
+    vop(8, ["eI2"], ["LX"], cp(T.LX[:], T.eI[:, 48:56]))
+    gop(8, [], ["idx"], iof(T.idx[:], [[16, 8]], 2560))
+    vop(8, ["pF", "idx"], ["idx"], ts(T.idx[:], T.idx[:], T.pF[:, 0:1], None, OP.add))
+    gop(96, [], ["Ld"], iof(T.Ld[:], [[16, 96]], 256))
+    vop(96, ["pF", "Ld"], ["Ld"], ts(T.Ld[:], T.Ld[:], T.pF[:, 0:1], None, OP.add))
+    vop(96, ["Ld"], ["Ld1"], ts(T.Ld1[:], T.Ld[:], 1.0, None, OP.add))
+    vop(1, ["pF"], ["pF2"], ts(T.pF[:, 1:2], T.pF[:, 0:1], 16.0, None, OP.mult))
+    vop(1, ["pF"], ["pFn"], ts(T.pF[:, 6:7], T.pF[:, 0:1], -1024.0, 15360.0, OP.mult, OP.add))
+    gop(8, [], ["EB"], iof(T.EB[:], [[256, 8]], 15))
+    vop(8, ["pF2", "EB"], ["EB"], ts(T.EB[:], T.EB[:], T.pF[:, 1:2], None, OP.add))
+    vop(1, ["pI"], ["pT1"], ts(T.pT[:, 8:9], T.pI[:, 0:1], 7, None, OP.bitwise_and))
+    vop(1, ["pI"], ["pT2"], ts(T.pT[:, 16:17], T.pI[:, 0:1], 16, None, OP.bitwise_and))
+    vop(1, ["pI"], ["pT3"], ts(T.pT[:, 24:25], T.pI[:, 0:1], 3, 1, OP.logical_shift_right, OP.bitwise_and))
+    vop(1, ["pT2"], ["pF3"], cp(T.pF[:, 3:4], T.pT[:, 16:17]))
+    vop(1, ["pT1", "pF3"], ["pF4"], ts(T.pF[:, 4:5], T.pT[:, 8:9], 32.0, T.pF[:, 3:4], OP.mult, OP.add))
+    vop(1, ["pT3", "pF4"], ["pF5"], tt(T.pF[:, 5:6], T.pT[:, 24:25], T.pF[:, 4:5], OP.add))
+    gop(8, [], ["eI3"], ioi(T.eI[:, 56:64], [[2, 8]], 0, 0))
+    vop(8, ["eI3", "pF5"], ["LP"], ts(T.LP[:], T.eI[:, 56:64], T.pF[:, 5:6], None, OP.add))
+    gop(128, ["onesB"], ["ntri"], sel(T.ntri[:], T.onesB[:], [[-1, 128]], OP.is_gt, 0, 1))
+    vop(128, ["ntri", "grp"], ["ntri"], tt(T.ntri[:], T.ntri[:], T.grp[:], OP.mult))
+    vop(128, ["ntri"], ["ntri"], ts(T.ntri[:], T.ntri[:], -1.0, None, OP.mult))
+    for t in range(R):
+        vop(128, [], ["stv%d" % t], fill(T.stv[:, 128 * t:128 * t + 128], float(32 * 8 ** t)))
+        vop(128, [], ["sts%d" % t], fill(T.sts[:, 128 * t:128 * t + 128], float(32 * 8 ** t)))
+    vop(2560, ["co0", "co1"], ["tmpI"], ts(T.tmpI[:], T.coI[:, 0:2560], 5, None, OP.logical_shift_right))
+    vop(2560, ["tmpI"], ["coH"], cp(T.coH[:], T.tmpI[:]))
+    vop(2560, ["co0", "co1"], ["tmpI"], ts(T.tmpI[:], T.coI[:, 0:2560], 31, None, OP.bitwise_and))
+    vop(2560, ["tmpI"], ["coL"], cp(T.coL[:], T.tmpI[:]))
+
+    def send(dst_rank, out, in_, sem, r):
+        dst = T.cores[dst_rank]
+        rid, pid, _ = topo.addr(dst)
+        m = sum(1 << e for e in topo.engines(core, dst)[:4])
+        return op("G", 0.6, r, [], [lambda: g.remote_dma(out, in_, T.sem[sem], T.sem.ls, pid, rid, m)], "none", 0)
+
+    for t in (1, 2, 3):
+        i = send((rank + t) % N, T.dls[:, 256 * t:256 * t + 256], T.dls[:, 0:256], "rdl%d" % t, ["dl0"])
+        op("R", 4.0, [], ["dl%d" % t], [], "rdl%d" % t, 4, True, order=[i])
+    for k in range(16):
+        if k % 2:
+            vop(256, ["dl0"], ["sh0_%d" % k], cp(T.sh0[:, k::16], T.dls[:, 0:256]), 0.5)
+        else:
+            sop(256, ["dl0"], ["sh0_%d" % k], act(T.sh0[:, k::16], T.dls[:, 0:256], AF.Copy))
+    hs = (0, 1)
+    for h in hs:
+        for q, nm in enumerate(("laI", "lbI")):
+            o = 16 * h + 8 * q
+            vop(8, [nm], ["abI%d%d" % (h, q)], cp(T.abI[:, o:o + 8], T[nm][:, 8 * h:8 * h + 8]))
+    cur, co_, cur_t = T.abI, 0, {(h, q): "abI%d%d" % (h, q) for h in hs for q in (0, 1)}
+
+    for t in range(R):
+        sh = T.sh0 if t % 2 == 0 else T.sh1
+        sht = ["sh%d_%d" % (t % 2, k) for k in range(16)]
+        if t:
+            for k in range(16):
+                gop(256, ["dl%d" % t], [sht[k]], sel(sh[:, k::16], T.dls[:, 256 * t:256 * t + 256], [[0, 256]], OP.is_ge, 1, 0))
+        no = 32 * t
+        for h in hs:
+            o = 16 * h
+            vop(16, [cur_t[h, 0], cur_t[h, 1]], ["abU%d" % h], cp(T.abU[:, o:o + 16], cur[:, co_ + o:co_ + o + 16]))
+            vg(256, ["abU%d" % h] + co_t[:2], ["df%d" % h], cp(T.df[:, 256 * h:256 * h + 256], T.coI[:, 0:2560].indirect(T.abU[:, o:o + 16])))
+            for nm in ("H", "L"):
+                sg(256, ["abU%d" % h, "co" + nm], ["df%s%d" % (nm, h)], act(T["df" + nm][:, 256 * h:256 * h + 256], T["co" + nm][:].indirect(T.abU[:, o:o + 16]), AF.Copy))
+
+        def second(step, h, q, lists, lo, Mb, mt, lt):
+            a, zt = 2048 * h + 512 * q, "z%d%d" % (h, q)
+            win = T.Xw[:, 0:2560].indirect(lists[:, lo + 32 * q:lo + 32 * q + 32])
+            if q in SPATH[step][h]:
+                gt, P = "gF%d%d" % (h, q), "P%d" % bank()
+                sg(512, x_t + [lt], [gt], act(T.gF[:, a:a + 512], win, AF.Copy))
+                pop(1024, ["ident", "nident", gt, mt], [P], [mm(T[P][:], T.nident[:], Mb[:, a:a + 512], True, False), mm(T[P][:], T.ident[:], T.gF[:, a:a + 512], False, True)])
+                sop(512, [], [P, "a" + zt], act(T.az[:, a:a + 512], T[P][:], AF.Abs))
+            else:
+                vg(512, x_t + [lt, mt], [zt], tt(T.z[:, a:a + 512], win, Mb[:, a:a + 512], OP.subtract))
+                sop(512, [zt], ["a" + zt], act(T.az[:, a:a + 512], T.z[:, a:a + 512], AF.Abs))
+
+        def moved(step, h, q, lists, lo, lt, Mb, mt):
+            a = 2048 * h + 512 * q
+            win = T.Xw[:, 0:2560].indirect(lists[:, lo + 32 * q:lo + 32 * q + 32])
+            if q in MPATH[step][h]:
+                gt, P = "gF%d%d" % (h, q), "P%d" % bank()
+                sg(512, x_t + [lt], [gt], act(T.gF[:, a:a + 512], win, AF.Copy))
+                pop(1024, ["ident", gt] + sht, [P], [mm(T[P][:], T.ident[:], sh[:, a:a + 512], True, False), mm(T[P][:], T.ident[:], T.gF[:, a:a + 512], False, True)])
+                vop(512, [], [P, mt], ts(Mb[:, a:a + 512], T[P][:], 0.0, 63.0, OP.max, OP.min))
+                return
+            vg(512, x_t + [lt] + sht, [mt], tt(Mb[:, a:a + 512], win, sh[:, a:a + 512], OP.add))
+            vop(512, [mt], [mt], ts(Mb[:, a:a + 512], Mb[:, a:a + 512], 0.0, 63.0, OP.max, OP.min), 0.5)
+
+        for h in hs:
+            X = lambda n, a=0, b=None, s=1, h=h: T[n][:, h * HALF[n] + a:h * HALF[n] + (HALF[n] if b is None else b):s]
+            K = lambda n, h=h: "%s_%d" % (n, h)
+            b, o, a0 = 256 * h, 16 * h, 2048 * h
+            for q in range(4):
+                moved(1, h, q, T.df, b, "df%d" % h, T.M, "M%d%d" % (h, q))
+            for q in range(4):
+                second(1, h, q, T.df, b + 128, T.M, "M%d%d" % (h, q), "df%d" % h)
+            azt = ["az%d%d" % (h, q) for q in range(4)]
+            f4 = [mm(T.P0[:], T.ident[:], T.cK[:, 0:512], True, False)]
+            for i, (tb, d) in enumerate((("dfH", 0), ("dfL", 0), ("dfH", 128), ("dfL", 128))):
+                f4.append(mm(T.P0[:, 128 * i:128 * i + 128], T[tb][:, b + d:b + d + 128], T.ident[:], False, False))
+            pop(1152, ["ident", "cK", "dfH%d" % h, "dfL%d" % h], ["P0", "P1"], f4 + [mm(T.P1[:, 0:128], T.ident[:], T.cK[:, 512:640], True, False)])
+            l = [T.az[:, a0 + k:a0 + 2048:16] for k in range(16)]
+            pop(1024, azt + ["g8p"], ["P0"], [mm(T.P0[:, k::16], l[k], T.g8p[:, 0:32], False, k == 15) for k in range(16)])
+            pop(1024, azt + ["g8p"], ["P1"], [mm(T.P1[:, k:128:16], l[k], T.g8p[:, 32:40], False, k == 15) for k in range(16)])
+            vop(512, ["segN"], [K("S") + "a", "P0"], scan(X("S", 0, 512), T.segN[:], T.P0[:], 1e9, OP.max, OP.min))
+            vop(128, ["segN"], [K("S") + "b", "P1"], scan(X("S", 512), T.segN[:, 0:128], T.P1[:, 0:128], 1e9, OP.max, OP.min))
+            vg(640, [K("S") + "a", K("S") + "b", "LE", "dm"], [K("B")], tt(X("B"), X("S").indirect(T.LE[:]), T.dm[:], OP.mult))
+            c32, c41, c1 = T.g8s[:, 0:8], T.g8s[:, 8:16], T.g8s[:, 16:24]
+            blk = [X("B", 128 * i, 128 * i + 128) for i in range(5)]
+            pop(768, [K("B"), "g8s"], ["P2"], [mm(T.P2[:, 0:8], blk[0], c32, True, False), mm(T.P2[:, 0:8], blk[4], c41, False, False), mm(T.P2[:, 0:8], blk[1], c1, False, True)])
+            pop(1024, [K("B"), "g8s"], ["P3"], [mm(T.P3[:, 0:8], blk[2], c32, True, False), mm(T.P3[:, 0:8], blk[4], c41, False, False), mm(T.P3[:, 0:8], blk[3], c1, False, True),
+                                                mm(T.P3[:, 8:16], blk[4], c1, True, True)])
+            vop(8, [], [K("dL"), "P2"], cp(X("dL"), T.P2[:, 0:8]))
+            al = T.al[:, 8 * h:8 * h + 8]
+            vop(8, [cur_t[h, 0]], [K("ta"), "P2"], tt(X("ta", 0, 8), T.P2[:, 0:8], cur[:, co_ + o:co_ + o + 8], OP.subtract))
+            vop(8, [cur_t[h, 1]], [K("tb"), "P3"], tt(X("ta", 8, 16), T.P3[:, 0:8], cur[:, co_ + o + 8:co_ + o + 16], OP.subtract))
+            vop(8, ["thr"], ["al%d" % h, "P3"], ts(al, T.P3[:, 8:16], T.thr[:, 0:1], None, OP.is_lt))
+            for q, x in ((0, K("ta")), (1, K("tb"))):
+                tq, u = X("ta", 8 * q, 8 * q + 8), o + 8 * q
+                vop(8, [x, "al%d" % h], [x], tt(tq, tq, al, OP.mult))
+                vop(8, [x, cur_t[h, q]], ["abo%d%d%d" % (t, h, q)], tt(T.abo[:, no + u:no + u + 8], tq, cur[:, co_ + u:co_ + u + 8], OP.add))
+        new_t = {(h, q): "abo%d%d%d" % (t, h, q) for h in hs for q in (0, 1)}
+        if t < R - 1:
+            i = send((rank + 1) % N, T.land[:, no:no + 32], T.abo[:, no:no + 32], "rab%d" % (t + 1), list(new_t.values()))
+            op("R", 4.0, [], ["land%d" % (t + 1)], [], "rab%d" % (t + 1), 4, True, order=[i])
+            vop(16, ["al0", "al1"], ["acc"], lambda: V.tensor_reduce(T.acc[:, 0:1], T.al[:], AxisListType.X, OP.add))
+            pop(256, ["acc", "onesF"], ["P3"], [mm(T.P3[:, 16:17], T.onesF[:], T.acc[:, 0:1], True, True)])
+            vop(1, [], ["acI", "P3"], ts(T.acJ[:, 0:1], T.P3[:, 16:17], -1.0, 2048.0, OP.mult, OP.add))
+            vop(1, ["acI"], ["acJ"], ts(T.acJ[:, 8:9], T.acJ[:, 0:1], 63, None, OP.bitwise_and))
+            vop(1, ["acJ", "th16"], ["thr"], ts(T.thr[:, 0:1], T.acJ[:, 8:9], 16.0, T.th16[:, 0:1], OP.mult, OP.add))
+        else:
+            for h in hs:
+                for q, y in enumerate((T.ya, T.yb)):
+                    u = no + 16 * h + 8 * q
+                    op("Y", 2.0, [new_t[h, q]], [], [lambda y=y, h=h, u=u: g.sync.dma_start(y[:, 8 * h:8 * h + 8], T.abo[:, u:u + 8])], "so", 16, True)
+
+        for h in hs:
+            X = lambda n, a=0, b=None, s=1, h=h: T[n][:, h * HALF[n] + a:h * HALF[n] + (HALF[n] if b is None else b):s]
+            K = lambda n, h=h: "%s_%d" % (n, h)
+            a0 = 2048 * h
+            vg(128, [K("dL")] + su_t[:2], [K("sT")], cp(X("sT"), T.suI[:, 0:2560].indirect(X("dL"))))
+            for q in range(4):
+                moved(2, h, q, T.sT, 128 * h, K("sT"), T.E, "E%d%d" % (h, q))
+            et, azt = ["E%d%d" % (h, q) for q in range(4)], ["az%d%d" % (h, q) for q in range(4)]
+            pop(2048, et + ["WT"], ["P4"], [mm(T.P4[:, 0:128], T.WT[:, 128 * j:128 * j + 128], T.E[:, a0 + j:a0 + 2048:16], j == 0, j == 15) for j in range(16)])
+            vop(128, [], [K("uI"), "P4"], cp(X("uI"), T.P4[:, 0:128]))
+            sop(128, [], [K("uL"), "P4"], act(X("uL"), T.P4[:, 0:128], AF.Copy, scale=37.0))
+            vop(128, [K("uI")], [K("uI")], ts(X("uI"), X("uI"), 4095, None, OP.bitwise_and))
+            vop(128, [K("uI")], [K("uA")], tt(X("uA"), X("uI"), X("uI"), OP.mult), 2)
+            vop(128, [K("uA")], [K("uA")], ts(X("uA"), X("uA"), 5, None, OP.logical_shift_right))
+            vop(128, [K("uA"), K("uL")], [K("uI")], tt(X("uI"), X("uA"), X("uL"), OP.add), 2)
+            vop(128, [K("uI")], [K("uI")], ts(X("uI"), X("uI"), 1023, None, OP.bitwise_and))
+            vop(128, [K("uI")], [K("nO")], cp(X("nO"), X("uI")))
+            vop(128, [K("uI"), "pFn"], [K("nP")], ts(X("nP"), X("uI"), T.pF[:, 6:7], None, OP.add))
+            for q in range(4):
+                second(2, h, q, T.nO, 128 * h, T.E, "E%d%d" % (h, q), K("nO"))
+            pop(512, [K("nP"), "identF"], ["P1"], [mm(T.P1[:, 128:256], X("nP"), T.identF[:], True, False)])
+            pop(1024, azt + ["g8p"], ["P1"], [mm(T.P1[:, 128 + j:256:16], T.az[:, a0 + j:a0 + 2048:16], T.g8p[:, 40:48], False, j == 15) for j in range(16)])
+            vop(128, ["segX"], [K("S") + "a", "P1"], scan(X("S", 0, 128), T.segX[:], T.P1[:, 128:256], 0.0, OP.min, OP.max))
+            vg(128, [K("S") + "a", "LE", "dm"], [K("B")], tt(X("B", 0, 128), X("S", 0, 128).indirect(T.LE[:, 0:8]), T.dm[:, 0:128], OP.mult))
+            pop(256, [K("B"), "g8"], ["P2"], [mm(T.P2[:, 16:24], X("B", 0, 128), T.g8[:], True, True)])
+            vop(8, [], [K("vI"), "P2"], cp(X("vI"), T.P2[:, 16:24]))
+            vop(8, [K("vI")], [K("nI")], ts(X("nI"), X("vI"), 1023, None, OP.bitwise_and))
+            vop(8, [K("vI")], [K("jI")], ts(X("jI"), X("vI"), 10, 15, OP.logical_shift_right, OP.bitwise_and))
+            vop(8, [K("jI"), "EB"], [K("jI")], tt(X("jI"), T.EB[:], X("jI"), OP.subtract))
+            vop(8, [K("jI")], [K("eO")], cp(X("eO"), X("jI")))
+            vg(128, et + [K("eO")], [K("eS")], cp(X("eS"), T.E[:, a0:a0 + 2048].indirect(X("eO"))))
+            vop(8, [K("nI"), "idx"], [K("nt")], tt(X("nt"), T.idx[:], X("nI"), OP.subtract))
+            vop(8, [K("nt"), "al%d" % h], [K("nt")], tt(X("nt"), X("nt"), T.al[:, 8 * h:8 * h + 8], OP.mult))
+            vop(8, [K("nt"), K("nI")], [K("nS")], tt(X("nS"), X("nI"), X("nt"), OP.add))
+            vg(128, [K("nS"), "LX", "dm"], [K("B")], tt(X("B", 0, 128), X("nS").indirect(T.LX[:]), T.dm[:, 0:128], OP.mult))
+            pop(512, [K("B"), "grpF"], ["P2"], [mm(T.P2[:, 128:256], T.grpF[:], X("B", 0, 128), True, True)])
+            sop(128, [], [K("nBs"), "P2"], act(X("nBs"), T.P2[:, 128:256], AF.Copy))
+            eqt = ["EQ%d%d" % (h, i) for i in range(8)]
+            vg(128, [K("nS"), "LX", K("nBs")], [eqt[7]], tt(X("EQ", 896), X("nS").indirect(T.LX[:]), X("nBs"), OP.is_equal))
+            vop(128, [eqt[7], "ltm"], [eqt[7]], tt(X("EQ", 896), X("EQ", 896), T.ltm[:], OP.mult), 2)
+            fs = [mm(T.P3[:, 128:256], T.grp[:], X("EQ", 896), True, False)]
+            for c in range(7):
+                s = 16 * (c + 1)
+                e = X("EQ", 128 * c + s, 128 * c + 128)
+                vop(128 - s, [K("nS"), K("nBs")], [eqt[c]], ts(e, X("nBs", s), X("nS", c, c + 1), None, OP.is_equal))
+                fs.append(mm(T.P3[:, 128 + s:256], T.grp[:], e, False, c == 6))
+            pop(640, eqt + ["grp"], ["P3"], fs)
+            vop(128, ["dm"], [K("B"), "P3"], tt(X("B", 0, 128), T.P3[:, 128:256], T.dm[:, 0:128], OP.mult))
+            vop(128, [K("B"), "seg1"], [K("S") + "b"], scan(X("S", 512), T.seg1[:, 0:128], X("B", 0, 128), 0.0, OP.mult, OP.add))
+            vop(8, [K("S") + "b"], [K("nl")], ts(X("nl"), X("S", 527, 640, 16), 0.5, None, OP.is_ge))
+            vop(8, [K("nS"), "idx"], [K("nt")], tt(X("nt"), T.idx[:], X("nS"), OP.subtract))
+            vop(8, [K("nt"), K("nl")], [K("nt")], tt(X("nt"), X("nt"), X("nl"), OP.mult))
+            vop(8, [K("nt"), K("nS")], [K("nl")], tt(X("nl"), X("nS"), X("nt"), OP.add))
+            for x in (0, 1):
+                vop(8, [K("nl")], [K("oD%d" % x)], cp(X("oD", x, 16, 2), X("nl")))
+            vop(8, [K("nl")], [K("oU")], cp(X("oU"), X("nl")))
+            vg(256, [K("oD0"), K("oD1")] + co_t, [K("T1")], cp(X("T1"), T.coI[:].indirect(X("oD"))))
+            vop(256, [K("T1")], [K("T2")], lambda X=X: V.transpose(X("T2"), X("T1")))
+            vg(128, [K("T2"), "LP"], [K("fL")], cp(X("fL"), X("T2").indirect(T.LP[:])))
+            for k in range(16):
+                off = X("fL", 8 * k, 8 * k + 8)
+                if k in FLAG_S[h]:
+                    sop(128, [K("fL"), "sts%d" % t], ["Fs%d" % h], act(T["Fs%d" % h][:].indirect(off), T.sts[:, 128 * t:128 * t + 128], AF.Silu), SC)
+                else:
+                    vop(128, [K("fL"), "stv%d" % t], ["Fv"], cp(T.Fv[:].indirect(off), T.stv[:, 128 * t:128 * t + 128]), SC)
+            sop(1536, ["Fs%d" % h], ["FsB%d" % h], act(T["FsB%d" % h][:], T["Fs%d" % h][:, 1024:2560], AF.Copy))
+        for h in (1, 0):
+            vop(128, ["eS_%d" % h, "oU_%d" % h], x_t, cp(T.Xw[:].indirect(T.oU[:, 8 * h:8 * h + 8]), T.eS[:, 128 * h:128 * h + 128]), SC)
+
+        F = lambda src, o, first, last: [mm(T.P4[:, 256:352], T.selX[:, 128 * r:128 * r + 128], src[:, o + r:o + 1536:16], first and r == 0, last and r == 15) for r in range(16)]
+        pop(1536, ["FsB0", "selX"], ["P4"], F(T.FsB0, 0, True, False))
+        for x in (0, 1):
+            gop(256, [], ["Vw%d" % x], iof(T["Vw%d" % x][:, 0:256], [[1, 256]], 2560))
+        pop(1536, ["FsB1", "selX"], ["P4"], F(T.FsB1, 0, False, False))
+        pop(1536, ["Fv", "selX"], ["P4"], F(T.Fv, 1024, False, True))
+        vop(96, [], ["Fn", "P4"], ts(T.Fn[:], T.P4[:, 256:352], 384.0 * 8 ** t, None, OP.is_ge))
+        vop(96, ["Fn", "Fp"], ["Fp"], tt(T.Fp[:], T.Fp[:], T.Fn[:], OP.max), 2)
+        vop(96, ["Fp", "one96"], ["Fi"], scan(T.Fi[:], T.one96[:], T.Fp[:], 0.0, OP.mult, OP.add), 0.5)
+        pop(192, ["Fp", "Fi", "ntri", "grp"], ["P7"], [mm(T.P7[:, 0:96], T.ntri[:], T.Fp[:], True, False), mm(T.P7[:, 0:96], T.grp[:], T.Fi[:], False, True)])
+        vop(96, ["Ld1"], ["s96", "P7"], tt(T.s96[:], T.P7[:, 0:96], T.Ld1[:], OP.subtract))
+        vop(96, [], ["t96", "P7"], ts(T.t96[:], T.P7[:, 0:96], 256.0, None, OP.is_le))
+        vop(96, ["t96", "Fp"], ["t96"], tt(T.t96[:], T.t96[:], T.Fp[:], OP.mult), 2)
+        vop(96, ["t96", "s96"], ["s96"], tt(T.s96[:], T.s96[:], T.t96[:], OP.mult), 2)
+        vop(96, ["s96", "Ld"], ["s96"], tt(T.s96[:], T.s96[:], T.Ld[:], OP.add), 2)
+        vop(96, ["s96"], ["Lv"], cp(T.Lv[:], T.s96[:]))
+        vop(768, ["Lv", "iotaV"], ["Vw0"], cp(T.Vw0[:].indirect(T.Lv[:, 0:48]), T.iotaV[:, 0:768]), SC)
+        sop(768, ["Lv", "iotaV"], ["Vw1"], act(T.Vw1[:].indirect(T.Lv[:, 48:96]), T.iotaV[:, 768:1536], AF.Silu), SC)
+        vop(96, ["t96", "Fp"], ["Fp"], tt(T.Fp[:], T.Fp[:], T.t96[:], OP.subtract), 2)
+        vop(256, ["Vw0", "Vw1"], ["vS"], tt(T.vS[:], T.Vw0[:, 0:256], T.Vw1[:, 0:256], OP.min), 2)
+        vop(256, ["vS", "dm"], ["vX"], tt(T.vX[:], T.vS[:], T.dm[:, 0:256], OP.mult), 2)
+        vop(256, ["vX", "seg1"], ["vS"], scan(T.vS[:], T.seg1[:], T.vX[:], 0.0, OP.mult, OP.add))
+        vop(16, ["vS"], ["vI"], cp(T.accI[:], T.vS[:, 15::16]))
+        vop(16, ["vI"], ["vL"], cp(T.vL[:], T.accI[:]))
+        vg(256, ["vL"] + su_t, ["sR"], cp(T.sR[:], T.suI[:].indirect(T.vL[:])))
+        for q in range(8):
+            a, h = 512 * q, q // 4
+            gt, zt, at = "gF%d%d" % (h, q % 4), "z%d%d" % (h, q % 4), "az%d%d" % (h, q % 4)
+            win = T.Xw[:, 0:2560].indirect(T.sR[:, 32 * q:32 * q + 32])
+            if q in REN_S:
+                sg(512, x_t + ["sR"], [gt], act(T.gF[:, a:a + 512], win, AF.Copy))
+            else:
+                vg(512, x_t + ["sR"], [gt], cp(T.gF[:, a:a + 512], win))
+            vop(512, [gt, "rX"], [zt], scan(T.z[:, a:a + 512], T.rX[:], T.gF[:, a:a + 512], 0.0, OP.min, OP.max), 0.5)
+            vop(512, [gt, "rN"], [at], scan(T.az[:, a:a + 512], T.rN[:], T.gF[:, a:a + 512], 64.0, OP.max, OP.min), 0.5)
+            if q % 4 == 3:
+                b = 2048 * h
+                vop(128, [x + "%d%d" % (h, i) for i in range(4) for x in ("z", "az")], ["rs%d" % h],
+                    tt(T.rs[:, 128 * h:128 * h + 128], T.z[:, b + 15:b + 2048:16], T.az[:, b + 15:b + 2048:16], OP.add), 2)
+        vop(256, ["rs0", "rs1"], ["rI"], ts(T.rI[:], T.rs[:], 0.5, -0.25, OP.mult, OP.add))
+        vop(256, ["rI", "vL"], x_t, cp(T.Xw[:].indirect(T.vL[:]), T.rI[:]), SC)
+        cur, co_, cur_t = T.land, no, {(h, q): "land%d" % (t + 1) for h in hs for q in (0, 1)}
+    for a in (0, 1280):
+        op("Y", 4.0, x_t, [], [lambda a=a: g.sync.dma_start(T.yx[:, a:a + 1280], T.Xw[:, a:a + 1280])], "so", 16, True)
+
+    if "o" not in ORDER:
+        ORDER["o"], ORDER["start"], ORDER["end"] = schedule(ops)
+        ORDER["ops"] = [(o["e"], o["c"]) for o in ops]
+    queue = {"V": V, "S": S, "PE": PE, "G": g, "Y": g.sync}
+    count, known = {}, {q: {} for q in queue}
+    for i in ORDER["o"]:
+        o = ops[i]
+        e, clk = o["e"], {}
+        if e != "R":
+            kn = known[e]
+            for d in reversed(o["hard"]):
+                x = ops[d]
+                if x["sem"] != "none" and kn.get(x["s"], 0) < x["n"]:
+                    queue[e].wait_ge(T.sem[x["s"]], x["n"])
+                    for s, v in x["clk"].items():
+                        kn[s] = max(kn.get(s, 0), v)
+            clk = dict(kn)
+        s = o["sem"] or esem[e]
+        inc = 16 if o["sem"] else 1
+        for f in o["f"]:
+            ins = f()
+            if s != "none":
+                ins.then_inc(T.sem[s], inc)
+                count[s] = count.get(s, 0) + inc
+        if e == "R":
+            count[s] = o["val"]
+        if s != "none":
+            o["s"], o["n"] = s, count[s]
+            clk[s] = count[s]
+        o["clk"] = clk
+    for s in SEMAPHORES:
+        if count.get(s, 0) > known["Y"].get(s, 0):
+            g.sync.wait_ge(T.sem[s], count[s])
+    g.wait_ge(T.sem.ls, 4 * 6)

@@ -3,29 +3,30 @@ from concourse.mybir import AluOpType as OP, AxisListType, ActivationFunctionTyp
 R = 4
 SCRATCH = {}
 for _n, _w, _t in [
-        ("Xw", 2816, "bfloat16"), ("coI", 2688, "int32"), ("coH", 2560, "bfloat16"), ("coL", 2560, "bfloat16"), ("tmpI", 2560, "int32"),
+        ("Xw", 2816, "bfloat16"), ("coI", 2560, "int32"), ("coH", 2560, "bfloat16"), ("coF", 2688, "float32"),
         ("suI", 2816, "int32"), ("sh0", 4096, "bfloat16"), ("sh1", 4096, "bfloat16"), ("dls", 1024, "bfloat16"),
         ("M", 4096, "bfloat16"), ("E", 4096, "bfloat16"), ("z", 4096, "bfloat16"), ("az", 4096, "bfloat16"), ("gF", 4096, "bfloat16"),
         ("Fv", 2688, "bfloat16"), ("Fs0", 2688, "float32"), ("Fs1", 2688, "float32"), ("FsB0", 1536, "bfloat16"), ("FsB1", 1536, "bfloat16"),
-        ("Vw0", 1792, "float32"), ("Vw1", 1792, "float32"), ("iotaV", 1536, "float32"),
-        ("ident", 128, "bfloat16"), ("nident", 128, "bfloat16"), ("identF", 128, "float32"), ("grp", 128, "bfloat16"), ("grpF", 128, "float32"),
+        ("Vw0", 3072, "float32"), ("Vw1", 3072, "float32"), ("iotaV", 1536, "float32"),
+        ("ident", 128, "bfloat16"), ("nident", 128, "bfloat16"), ("nid32", 128, "bfloat16"), ("nid4k", 128, "bfloat16"), ("idBig", 128, "bfloat16"),
+        ("c4k", 96, "bfloat16"), ("dmI", 128, "float32"), ("ta", 32, "float32"), ("identF", 128, "float32"), ("grp", 128, "bfloat16"), ("grpF", 128, "float32"),
         ("onesF", 128, "float32"), ("onesB", 128, "bfloat16"), ("ntri", 128, "bfloat16"), ("selX", 2048, "bfloat16"), ("WT", 2048, "bfloat16"),
         ("g8", 8, "float32"), ("g8s", 24, "float32"), ("g8p", 48, "bfloat16"), ("cK", 640, "bfloat16"),
         ("jm", 1024, "float32"), ("segN", 512, "float32"), ("segX", 128, "float32"), ("seg1", 256, "float32"), ("rN", 512, "bfloat16"), ("rX", 512, "bfloat16"),
         ("dm", 640, "float32"), ("ltm", 128, "bfloat16"), ("pI", 8, "int32"), ("pT", 32, "int32"), ("pF", 8, "float32"),
-        ("eI", 64, "int32"), ("LE", 40, "uint16"), ("LX", 8, "uint16"), ("LP", 8, "uint16"), ("Ld", 96, "float32"), ("Ld1", 96, "float32"),
+        ("eI", 64, "int32"), ("LE", 40, "uint16"), ("LX", 8, "uint16"), ("LP", 8, "uint16"), ("Ld1", 96, "float32"),
         ("idx", 8, "float32"), ("EB", 8, "float32"), ("one96", 96, "bfloat16"),
         ("stv", 512, "bfloat16"), ("sts", 512, "float32"), ("wt_", 8, "bfloat16"), ("wtF", 8, "float32"), ("thI", 8, "int32"), ("thF", 8, "float32"),
         ("thr", 8, "float32"), ("th16", 8, "float32"), ("gT", 128, "float32"), ("laI", 16, "int32"), ("lbI", 16, "int32"),
         ("abI", 32, "float32"), ("land", 128, "float32"), ("abo", 128, "float32"), ("abU", 32, "uint16"),
-        ("al", 16, "float32"), ("acc", 8, "float32"), ("acJ", 16, "int32"), ("accI", 16, "int32"),
-        ("df", 512, "uint16"), ("dfH", 512, "bfloat16"), ("dfL", 512, "bfloat16"),
-        ("Fp", 96, "bfloat16"), ("Fn", 96, "bfloat16"), ("Fi", 96, "bfloat16"), ("t96", 96, "float32"), ("s96", 96, "float32"), ("Lv", 96, "uint16"),
+        ("al", 16, "float32"), ("acc", 8, "float32"), ("acJ", 16, "int32"),
+        ("df", 512, "uint16"), ("dfH", 512, "bfloat16"), ("dfF", 512, "float32"),
+        ("Fp", 96, "bfloat16"), ("Fc", 96, "bfloat16"), ("Fi", 96, "bfloat16"), ("t96", 96, "float32"), ("s96", 96, "float32"), ("Lv", 96, "uint16"),
         ("vX", 256, "float32"), ("vS", 256, "float32"), ("vL", 16, "uint16"), ("sR", 256, "uint16"), ("rs", 256, "float32"), ("rI", 256, "int32")]:
     SCRATCH[_n] = ("sbuf", [128, _w], _t)
 HALF = {}
-for _n, _w, _t in [("S", 640, "float32"), ("B", 640, "float32"), ("dL", 8, "uint16"), ("ta", 16, "float32"), ("sT", 128, "uint16"),
-                   ("uI", 128, "int32"), ("uA", 128, "int32"), ("uL", 128, "float32"), ("nO", 128, "uint16"), ("nP", 128, "float32"),
+for _n, _w, _t in [("S", 640, "float32"), ("B", 640, "float32"), ("dL", 8, "uint16"), ("sT", 128, "uint16"),
+                   ("uI", 128, "int32"), ("uA", 128, "int32"), ("uB", 128, "int32"), ("nO", 128, "uint16"), ("nP", 128, "float32"),
                    ("vI", 8, "int32"), ("nI", 8, "int32"), ("jI", 8, "int32"), ("eO", 8, "uint16"), ("nS", 8, "float32"), ("nt", 8, "float32"), ("nl", 8, "float32"),
                    ("nBs", 128, "float32"), ("EQ", 1024, "bfloat16"), ("oU", 8, "uint16"), ("oD", 16, "uint16"), ("T1", 256, "float32"),
                    ("T2", 256, "float32"), ("fL", 128, "uint16"), ("eS", 128, "bfloat16")]:
@@ -37,10 +38,10 @@ for _b in range(8):
 LOADS = ["la", "lb", "dl", "co0", "co1", "x0", "x1", "su0", "su1", "wt", "th"]
 SEMAPHORES = ["sv", "ss", "sp", "sg", "ls", "so"] + ["ld_" + n for n in LOADS] + ["rdl%d" % t for t in (1, 2, 3)] + ["rab%d" % t for t in (1, 2, 3)]
 
-CY, WAKE, LAM, GA, SC = 0.83e-3, 0.1, 0.02, 1.5, 3.5
-SPATH = {1: ((1, 3), (1, 3)), 2: ((1, 3), (1, 3))}
-MPATH = {1: ((1, 3), (3,)), 2: ((3,), (3,))}
-FLAG_S = (tuple(range(12)), tuple(range(6)))
+CY, WAKE, LAM, GA, SC = 0.83e-3, 0.1, 0.0, 1.5, 3.5
+SPATH = {1: ((1, 3), (1, 2, 3)), 2: ((1, 3), (1, 3))}
+MPATH = {1: ((1, 3), (3,)), 2: ((), (3,))}
+FLAG_S = (tuple(range(10)), tuple(range(5)))
 REN_S = (1, 2, 3, 4, 5, 6, 7)
 ORDER = {}
 
@@ -138,7 +139,7 @@ def rank_program(g, core, T, topo):
     load("Y", "th", 3, ["thI"], T.thI[0:8, 0:1], T.th[:])
     load("Y", "su0", 12, ["su0"], T.suI[:, 0:1280], T.su[:, 0:1280])
     load("Y", "su1", 12, ["su1"], T.suI[:, 1280:2560], T.su[:, 1280:2560])
-    co_t, su_t, x_t = ["co0", "co1", "co2"], ["su0", "su1", "su2"], ["X", "Xa", "Xb"]
+    co_t, su_t, x_t = ["co0", "co1"], ["su0", "su1", "su2"], ["X", "Xa", "Xb"]
 
     gop(1, [], ["pI"], ioi(T.pI[:, 0:1], [[0, 1]], 0, 1))
     gop(256, [], ["jm"], iof(T.jm[:], [[0, 64], [1, 16]], 0))
@@ -151,15 +152,19 @@ def rank_program(g, core, T, topo):
     vop(128, [], ["onesB"], fill(T.onesB[:], 1.0))
     vop(128, [], ["onesF"], fill(T.onesF[:], 1.0))
     gop(128, ["onesB"], ["ident"], sel(T.ident[:], T.onesB[:], [[-1, 128]], OP.is_equal, 0, 1))
-    vop(128, ["ident"], ["nident"], ts(T.nident[:], T.ident[:], -1.0, None, OP.mult))
+    for nm, c in (("nident", -1.0), ("nid32", -32.0), ("nid4k", -4096.0), ("idBig", 1048576.0)):
+        vop(128, ["ident"], [nm], ts(T[nm][:], T.ident[:], c, None, OP.mult))
+    vop(96, [], ["c4k"], fill(T.c4k[:], 4096.0))
+    gop(128, [], ["dmI"], iof(T.dmI[:], [[1, 128]], 2560))
+    vop(128, ["dmI", "dm"], ["dmI"], tt(T.dmI[:], T.dmI[:], T.dm[:, 0:128], OP.mult), 2)
     gop(8, ["onesF"], ["g8"], sel(T.g8[:], T.onesF[:, 0:8], [[-16, 8]], OP.is_ge, 0, 1))
     gop(8, ["g8"], ["g8"], sel(T.g8[:], T.g8[:], [[16, 8]], OP.is_ge, 15, -1))
-    for i, s in enumerate((2048.0, 512.0, 2048.0, 512.0, 16.0, 16384.0)):
+    for i, s in enumerate((2048.0, 512.0, 16.0, 2048.0, 512.0, 16384.0)):
         vop(8, ["g8"], ["g8p"], ts(T.g8p[:, 8 * i:8 * i + 8], T.g8[:], s, None, OP.mult))
     for i, s in enumerate((32.0, -4128.0, 1.0)):
         vop(8, ["g8"], ["g8s"], ts(T.g8s[:, 8 * i:8 * i + 8], T.g8[:], s, None, OP.mult))
-    for i, s in enumerate((128, 32, 128, 32, 1)):
-        gop(128, [], ["cK"], iof(T.cK[:, 128 * i:128 * i + 128], [[0, 8], [s, 16]], 0))
+    for i, (s, v) in enumerate(((128, -160), (32, 5120), (1, 0), (128, -160), (32, 5120))):
+        gop(128, [], ["cK"], iof(T.cK[:, 128 * i:128 * i + 128], [[0, 8], [s, 16]], v))
     gop(128, ["onesF"], ["grpF"], sel(T.grpF[:], T.onesF[:], [[-16, 8], [0, 16]], OP.is_ge, 0, 1))
     gop(128, ["grpF"], ["grpF"], sel(T.grpF[:], T.grpF[:], [[16, 8], [0, 16]], OP.is_ge, 15, -1))
     vop(128, ["grpF"], ["grp"], cp(T.grp[:], T.grpF[:]))
@@ -179,20 +184,20 @@ def rank_program(g, core, T, topo):
     vop(512, ["jm"], ["rX"], ts(T.rX[:], T.jm[:, 0:512], 0.0, 64.0, OP.is_gt, OP.mult))
     vop(128, ["jm", "pF"], ["ltm"], ts(T.ltm[:], T.jm[:, 0:128], T.pF[:, 0:1], None, OP.is_gt))
     vop(96, [], ["one96"], fill(T.one96[:], 1.0))
-    vop(96, [], ["Fp"], fill(T.Fp[:], 0.0))
+    vop(96, [], ["Fc"], fill(T.Fc[:], 0.0))
     vop(2688, [], ["Fv"], fill(T.Fv[:], 0.0), 0.5)
     for h in (0, 1):
         gop(2688, [], ["Fs%d" % h], iof(T["Fs%d" % h][:], [[0, 2688]], 0))
     vop(256, [], ["su2"], fill(T.suI[:, 2560:2816], 0))
-    gop(128, [], ["co2"], ioi(T.coI[:, 2560:2688], [[1, 128]], 2560, 0))
+    gop(128, [], ["coF2"], iof(T.coF[:, 2560:2688], [[1, 128]], 2560))
     gop(1536, [], ["iotaV"], iof(T.iotaV[:], [[1, 1536]], 1024))
+    sop(1536, ["iotaV"], ["iotaV"], act(T.iotaV[:], T.iotaV[:], AF.Identity, bias=0.25))
     gop(8, [], ["eI2"], ioi(T.eI[:, 48:56], [[1, 8]], 0, 0))
     vop(8, ["eI2"], ["LX"], cp(T.LX[:], T.eI[:, 48:56]))
     gop(8, [], ["idx"], iof(T.idx[:], [[16, 8]], 2560))
     vop(8, ["pF", "idx"], ["idx"], ts(T.idx[:], T.idx[:], T.pF[:, 0:1], None, OP.add))
-    gop(96, [], ["Ld"], iof(T.Ld[:], [[16, 96]], 256))
-    vop(96, ["pF", "Ld"], ["Ld"], ts(T.Ld[:], T.Ld[:], T.pF[:, 0:1], None, OP.add))
-    vop(96, ["Ld"], ["Ld1"], ts(T.Ld1[:], T.Ld[:], 1.0, None, OP.add))
+    gop(96, [], ["Ld1"], iof(T.Ld1[:], [[16, 96]], 1537))
+    vop(96, ["pF", "Ld1"], ["Ld1"], ts(T.Ld1[:], T.Ld1[:], T.pF[:, 0:1], None, OP.add))
     vop(1, ["pF"], ["pF2"], ts(T.pF[:, 1:2], T.pF[:, 0:1], 16.0, None, OP.mult))
     vop(1, ["pF"], ["pFn"], ts(T.pF[:, 6:7], T.pF[:, 0:1], -1024.0, 15360.0, OP.mult, OP.add))
     gop(8, [], ["EB"], iof(T.EB[:], [[256, 8]], 15))
@@ -211,10 +216,9 @@ def rank_program(g, core, T, topo):
     for t in range(R):
         vop(128, [], ["stv%d" % t], fill(T.stv[:, 128 * t:128 * t + 128], float(32 * 8 ** t)))
         vop(128, [], ["sts%d" % t], fill(T.sts[:, 128 * t:128 * t + 128], float(32 * 8 ** t)))
-    vop(2560, ["co0", "co1"], ["tmpI"], ts(T.tmpI[:], T.coI[:, 0:2560], 5, None, OP.logical_shift_right))
-    vop(2560, ["tmpI"], ["coH"], cp(T.coH[:], T.tmpI[:]))
-    vop(2560, ["co0", "co1"], ["tmpI"], ts(T.tmpI[:], T.coI[:, 0:2560], 31, None, OP.bitwise_and))
-    vop(2560, ["tmpI"], ["coL"], cp(T.coL[:], T.tmpI[:]))
+    for x in (0, 1):
+        vop(1280, ["co%d" % x], ["coF%d" % x], cp(T.coF[:, 1280 * x:1280 * x + 1280], T.coI[:, 1280 * x:1280 * x + 1280]))
+        sop(1280, ["coF%d" % x], ["coH%d" % x], act(T.coH[:, 1280 * x:1280 * x + 1280], T.coF[:, 1280 * x:1280 * x + 1280], AF.Identity, scale=0.03125, bias=159.515625))
 
     def send(dst_rank, out, in_, sem, r):
         dst = T.cores[dst_rank]
@@ -231,11 +235,9 @@ def rank_program(g, core, T, topo):
         else:
             sop(256, ["dl0"], ["sh0_%d" % k], act(T.sh0[:, k::16], T.dls[:, 0:256], AF.Copy))
     hs = (0, 1)
-    for h in hs:
-        for q, nm in enumerate(("laI", "lbI")):
-            o = 16 * h + 8 * q
-            vop(8, [nm], ["abI%d%d" % (h, q)], cp(T.abI[:, o:o + 8], T[nm][:, 8 * h:8 * h + 8]))
-    cur, co_, cur_t = T.abI, 0, {(h, q): "abI%d%d" % (h, q) for h in hs for q in (0, 1)}
+    for q, nm in enumerate(("laI", "lbI")):
+        vop(16, [nm], ["abI%d" % q], cp(T.abI[:, 16 * q:16 * q + 16], T[nm][:]))
+    cur, co_, cur_t = T.abI, 0, ["abI0", "abI1"]
 
     for t in range(R):
         sh = T.sh0 if t % 2 == 0 else T.sh1
@@ -244,12 +246,10 @@ def rank_program(g, core, T, topo):
             for k in range(16):
                 gop(256, ["dl%d" % t], [sht[k]], sel(sh[:, k::16], T.dls[:, 256 * t:256 * t + 256], [[0, 256]], OP.is_ge, 1, 0))
         no = 32 * t
-        for h in hs:
-            o = 16 * h
-            vop(16, [cur_t[h, 0], cur_t[h, 1]], ["abU%d" % h], cp(T.abU[:, o:o + 16], cur[:, co_ + o:co_ + o + 16]))
-            vg(256, ["abU%d" % h] + co_t[:2], ["df%d" % h], cp(T.df[:, 256 * h:256 * h + 256], T.coI[:, 0:2560].indirect(T.abU[:, o:o + 16])))
-            for nm in ("H", "L"):
-                sg(256, ["abU%d" % h, "co" + nm], ["df%s%d" % (nm, h)], act(T["df" + nm][:, 256 * h:256 * h + 256], T["co" + nm][:].indirect(T.abU[:, o:o + 16]), AF.Copy))
+        vop(32, cur_t, ["abU"], cp(T.abU[:], cur[:, co_:co_ + 32]))
+        vg(512, ["abU"] + co_t, ["df"], cp(T.df[:], T.coI[:].indirect(T.abU[:])))
+        for nm in ("H", "F"):
+            sg(512, ["abU", "co%s0" % nm, "co%s1" % nm], ["df" + nm], act(T["df" + nm][:], T["co" + nm][:, 0:2560].indirect(T.abU[:]), AF.Copy))
 
         def second(step, h, q, lists, lo, Mb, mt, lt):
             a, zt = 2048 * h + 512 * q, "z%d%d" % (h, q)
@@ -278,50 +278,48 @@ def rank_program(g, core, T, topo):
         for h in hs:
             X = lambda n, a=0, b=None, s=1, h=h: T[n][:, h * HALF[n] + a:h * HALF[n] + (HALF[n] if b is None else b):s]
             K = lambda n, h=h: "%s_%d" % (n, h)
-            b, o, a0 = 256 * h, 16 * h, 2048 * h
+            b, a0 = 128 * h, 2048 * h
             for q in range(4):
-                moved(1, h, q, T.df, b, "df%d" % h, T.M, "M%d%d" % (h, q))
+                moved(1, h, q, T.df, b, "df", T.M, "M%d%d" % (h, q))
             for q in range(4):
-                second(1, h, q, T.df, b + 128, T.M, "M%d%d" % (h, q), "df%d" % h)
+                second(1, h, q, T.df, b + 256, T.M, "M%d%d" % (h, q), "df")
             azt = ["az%d%d" % (h, q) for q in range(4)]
-            f4 = [mm(T.P0[:], T.ident[:], T.cK[:, 0:512], True, False)]
-            for i, (tb, d) in enumerate((("dfH", 0), ("dfL", 0), ("dfH", 128), ("dfL", 128))):
-                f4.append(mm(T.P0[:, 128 * i:128 * i + 128], T[tb][:, b + d:b + d + 128], T.ident[:], False, False))
-            pop(1152, ["ident", "cK", "dfH%d" % h, "dfL%d" % h], ["P0", "P1"], f4 + [mm(T.P1[:, 0:128], T.ident[:], T.cK[:, 512:640], True, False)])
+            for P, w, c0, d in (("P0", 384, 0, b), ("P1", 256, 384, b + 256)):
+                lh, lf = T.dfH[:, d:d + 128], T.dfF[:, d:d + 128]
+                pop(w + 768, ["ident", "identF", "nid32", "cK", "dfH", "dfF"], [P], [
+                    mm(T[P][:, 0:w], T.ident[:], T.cK[:, c0:c0 + w], True, False), mm(T[P][:, 0:128], lh, T.ident[:], False, False),
+                    mm(T[P][:, 128:256], lf, T.identF[:], False, False), mm(T[P][:, 128:256], lh, T.nid32[:], False, False)])
             l = [T.az[:, a0 + k:a0 + 2048:16] for k in range(16)]
-            pop(1024, azt + ["g8p"], ["P0"], [mm(T.P0[:, k::16], l[k], T.g8p[:, 0:32], False, k == 15) for k in range(16)])
-            pop(1024, azt + ["g8p"], ["P1"], [mm(T.P1[:, k:128:16], l[k], T.g8p[:, 32:40], False, k == 15) for k in range(16)])
-            vop(512, ["segN"], [K("S") + "a", "P0"], scan(X("S", 0, 512), T.segN[:], T.P0[:], 1e9, OP.max, OP.min))
-            vop(128, ["segN"], [K("S") + "b", "P1"], scan(X("S", 512), T.segN[:, 0:128], T.P1[:, 0:128], 1e9, OP.max, OP.min))
-            vg(640, [K("S") + "a", K("S") + "b", "LE", "dm"], [K("B")], tt(X("B"), X("S").indirect(T.LE[:]), T.dm[:], OP.mult))
+            pop(1024, azt + ["g8p"], ["P0"], [mm(T.P0[:, k:384:16], l[k], T.g8p[:, 0:24], False, k == 15) for k in range(16)])
+            pop(1024, azt + ["g8p"], ["P1"], [mm(T.P1[:, k:256:16], l[k], T.g8p[:, 24:40], False, k == 15) for k in range(16)])
+            vop(384, ["segN"], [K("S") + "a", "P0"], scan(X("S", 0, 384), T.segN[:, 0:384], T.P0[:, 0:384], 1e9, OP.max, OP.min))
+            vg(384, [K("S") + "a", "LE", "dm"], [K("B")], tt(X("B", 0, 384), X("S", 0, 384).indirect(T.LE[:, 0:24]), T.dm[:, 0:384], OP.mult))
+            vop(256, ["segN"], [K("S") + "b", "P1"], scan(X("S", 384), T.segN[:, 0:256], T.P1[:, 0:256], 1e9, OP.max, OP.min))
+            vg(256, [K("S") + "b", "LE", "dm"], [K("B") + "b"], tt(X("B", 384), X("S", 384).indirect(T.LE[:, 0:16]), T.dm[:, 0:256], OP.mult))
             c32, c41, c1 = T.g8s[:, 0:8], T.g8s[:, 8:16], T.g8s[:, 16:24]
             blk = [X("B", 128 * i, 128 * i + 128) for i in range(5)]
-            pop(768, [K("B"), "g8s"], ["P2"], [mm(T.P2[:, 0:8], blk[0], c32, True, False), mm(T.P2[:, 0:8], blk[4], c41, False, False), mm(T.P2[:, 0:8], blk[1], c1, False, True)])
-            pop(1024, [K("B"), "g8s"], ["P3"], [mm(T.P3[:, 0:8], blk[2], c32, True, False), mm(T.P3[:, 0:8], blk[4], c41, False, False), mm(T.P3[:, 0:8], blk[3], c1, False, True),
-                                                mm(T.P3[:, 8:16], blk[4], c1, True, True)])
-            vop(8, [], [K("dL"), "P2"], cp(X("dL"), T.P2[:, 0:8]))
-            al = T.al[:, 8 * h:8 * h + 8]
-            vop(8, [cur_t[h, 0]], [K("ta"), "P2"], tt(X("ta", 0, 8), T.P2[:, 0:8], cur[:, co_ + o:co_ + o + 8], OP.subtract))
-            vop(8, [cur_t[h, 1]], [K("tb"), "P3"], tt(X("ta", 8, 16), T.P3[:, 0:8], cur[:, co_ + o + 8:co_ + o + 16], OP.subtract))
-            vop(8, ["thr"], ["al%d" % h, "P3"], ts(al, T.P3[:, 8:16], T.thr[:, 0:1], None, OP.is_lt))
-            for q, x in ((0, K("ta")), (1, K("tb"))):
-                tq, u = X("ta", 8 * q, 8 * q + 8), o + 8 * q
-                vop(8, [x, "al%d" % h], [x], tt(tq, tq, al, OP.mult))
-                vop(8, [x, cur_t[h, q]], ["abo%d%d%d" % (t, h, q)], tt(T.abo[:, no + u:no + u + 8], tq, cur[:, co_ + u:co_ + u + 8], OP.add))
-        new_t = {(h, q): "abo%d%d%d" % (t, h, q) for h in hs for q in (0, 1)}
+            pd, pf, pk = T.P2[:, 8 * h:8 * h + 8], T.P3[:, 8 * h:8 * h + 8], T.P3[:, 16 + 8 * h:24 + 8 * h]
+            pop(768, [K("B"), "g8s"], ["P2"], [mm(pd, blk[0], c32, True, False), mm(pd, blk[2], c41, False, False), mm(pd, blk[1], c1, False, True)])
+            pop(1024, [K("B"), K("B") + "b", "g8s"], ["P3"], [mm(pf, blk[3], c32, True, False), mm(pf, blk[2], c41, False, False), mm(pf, blk[4], c1, False, True), mm(pk, blk[2], c1, True, True)])
+            vop(8, [], [K("dL"), "P2"], cp(X("dL"), pd))
+        vop(16, ["thr"], ["al", "P3"], ts(T.al[:], T.P3[:, 16:32], T.thr[:, 0:1], None, OP.is_lt))
+        for q, P in ((0, "P2"), (1, "P3")):
+            tq = T.ta[:, 16 * q:16 * q + 16]
+            vop(16, cur_t, ["ta%d" % q, P], tt(tq, T[P][:, 0:16], cur[:, co_ + 16 * q:co_ + 16 * q + 16], OP.subtract))
+            vop(16, ["ta%d" % q, "al"], ["ta%d" % q], tt(tq, tq, T.al[:], OP.mult))
+        vop(32, ["ta0", "ta1"] + cur_t, ["abo%d" % t], tt(T.abo[:, no:no + 32], T.ta[:], cur[:, co_:co_ + 32], OP.add))
         if t < R - 1:
-            i = send((rank + 1) % N, T.land[:, no:no + 32], T.abo[:, no:no + 32], "rab%d" % (t + 1), list(new_t.values()))
+            i = send((rank + 1) % N, T.land[:, no:no + 32], T.abo[:, no:no + 32], "rab%d" % (t + 1), ["abo%d" % t])
             op("R", 4.0, [], ["land%d" % (t + 1)], [], "rab%d" % (t + 1), 4, True, order=[i])
-            vop(16, ["al0", "al1"], ["acc"], lambda: V.tensor_reduce(T.acc[:, 0:1], T.al[:], AxisListType.X, OP.add))
-            pop(256, ["acc", "onesF"], ["P3"], [mm(T.P3[:, 16:17], T.onesF[:], T.acc[:, 0:1], True, True)])
-            vop(1, [], ["acI", "P3"], ts(T.acJ[:, 0:1], T.P3[:, 16:17], -1.0, 2048.0, OP.mult, OP.add))
+            vop(16, ["al"], ["acc"], lambda: V.tensor_reduce(T.acc[:, 0:1], T.al[:], AxisListType.X, OP.add))
+            pop(256, ["acc", "onesF"], ["P3"], [mm(T.P3[:, 32:33], T.onesF[:], T.acc[:, 0:1], True, True)])
+            vop(1, [], ["acI", "P3"], ts(T.acJ[:, 0:1], T.P3[:, 32:33], -1.0, 2048.0, OP.mult, OP.add))
             vop(1, ["acI"], ["acJ"], ts(T.acJ[:, 8:9], T.acJ[:, 0:1], 63, None, OP.bitwise_and))
             vop(1, ["acJ", "th16"], ["thr"], ts(T.thr[:, 0:1], T.acJ[:, 8:9], 16.0, T.th16[:, 0:1], OP.mult, OP.add))
         else:
-            for h in hs:
-                for q, y in enumerate((T.ya, T.yb)):
-                    u = no + 16 * h + 8 * q
-                    op("Y", 2.0, [new_t[h, q]], [], [lambda y=y, h=h, u=u: g.sync.dma_start(y[:, 8 * h:8 * h + 8], T.abo[:, u:u + 8])], "so", 16, True)
+            for q, y in enumerate((T.ya, T.yb)):
+                u = no + 16 * q
+                op("Y", 2.0, ["abo%d" % t], [], [lambda y=y, u=u: g.sync.dma_start(y[:], T.abo[:, u:u + 16])], "so", 16, True)
 
         for h in hs:
             X = lambda n, a=0, b=None, s=1, h=h: T[n][:, h * HALF[n] + a:h * HALF[n] + (HALF[n] if b is None else b):s]
@@ -331,21 +329,21 @@ def rank_program(g, core, T, topo):
             for q in range(4):
                 moved(2, h, q, T.sT, 128 * h, K("sT"), T.E, "E%d%d" % (h, q))
             et, azt = ["E%d%d" % (h, q) for q in range(4)], ["az%d%d" % (h, q) for q in range(4)]
-            pop(2048, et + ["WT"], ["P4"], [mm(T.P4[:, 0:128], T.WT[:, 128 * j:128 * j + 128], T.E[:, a0 + j:a0 + 2048:16], j == 0, j == 15) for j in range(16)])
+            for x in (0, 1):
+                pop(1024, et[2 * x:2 * x + 2] + ["WT"], ["P4"], [mm(T.P4[:, 64 * x:64 * x + 64], T.WT[:, 128 * j:128 * j + 128], T.E[:, a0 + 1024 * x + j:a0 + 1024 * x + 1024:16], j == 0, j == 15) for j in range(16)])
             vop(128, [], [K("uI"), "P4"], cp(X("uI"), T.P4[:, 0:128]))
-            sop(128, [], [K("uL"), "P4"], act(X("uL"), T.P4[:, 0:128], AF.Copy, scale=37.0))
             vop(128, [K("uI")], [K("uI")], ts(X("uI"), X("uI"), 4095, None, OP.bitwise_and))
-            vop(128, [K("uI")], [K("uA")], tt(X("uA"), X("uI"), X("uI"), OP.mult), 2)
-            vop(128, [K("uA")], [K("uA")], ts(X("uA"), X("uA"), 5, None, OP.logical_shift_right))
-            vop(128, [K("uA"), K("uL")], [K("uI")], tt(X("uI"), X("uA"), X("uL"), OP.add), 2)
-            vop(128, [K("uI")], [K("uI")], ts(X("uI"), X("uI"), 1023, None, OP.bitwise_and))
+            vop(128, [K("uI")], [K("uA")], ts(X("uA"), X("uI"), -2048.0, None, OP.add))
+            vop(128, [K("uI")], [K("uB")], ts(X("uB"), X("uI"), 3232.0, None, OP.add))
+            vop(128, [K("uA"), K("uB")], [K("uA")], tt(X("uA"), X("uA"), X("uB"), OP.mult), 2)
+            vop(128, [K("uA")], [K("uI")], ts(X("uI"), X("uA"), 5, 1023, OP.arith_shift_right, OP.bitwise_and))
             vop(128, [K("uI")], [K("nO")], cp(X("nO"), X("uI")))
             vop(128, [K("uI"), "pFn"], [K("nP")], ts(X("nP"), X("uI"), T.pF[:, 6:7], None, OP.add))
             for q in range(4):
                 second(2, h, q, T.nO, 128 * h, T.E, "E%d%d" % (h, q), K("nO"))
-            pop(512, [K("nP"), "identF"], ["P1"], [mm(T.P1[:, 128:256], X("nP"), T.identF[:], True, False)])
-            pop(1024, azt + ["g8p"], ["P1"], [mm(T.P1[:, 128 + j:256:16], T.az[:, a0 + j:a0 + 2048:16], T.g8p[:, 40:48], False, j == 15) for j in range(16)])
-            vop(128, ["segX"], [K("S") + "a", "P1"], scan(X("S", 0, 128), T.segX[:], T.P1[:, 128:256], 0.0, OP.min, OP.max))
+            pop(512, [K("nP"), "identF"], ["P1"], [mm(T.P1[:, 256:384], X("nP"), T.identF[:], True, False)])
+            pop(1024, azt + ["g8p"], ["P1"], [mm(T.P1[:, 256 + j:384:16], T.az[:, a0 + j:a0 + 2048:16], T.g8p[:, 40:48], False, j == 15) for j in range(16)])
+            vop(128, ["segX"], [K("S") + "a", "P1"], scan(X("S", 0, 128), T.segX[:], T.P1[:, 256:384], 0.0, OP.min, OP.max))
             vg(128, [K("S") + "a", "LE", "dm"], [K("B")], tt(X("B", 0, 128), X("S", 0, 128).indirect(T.LE[:, 0:8]), T.dm[:, 0:128], OP.mult))
             pop(256, [K("B"), "g8"], ["P2"], [mm(T.P2[:, 16:24], X("B", 0, 128), T.g8[:], True, True)])
             vop(8, [], [K("vI"), "P2"], cp(X("vI"), T.P2[:, 16:24]))
@@ -353,33 +351,32 @@ def rank_program(g, core, T, topo):
             vop(8, [K("vI")], [K("jI")], ts(X("jI"), X("vI"), 10, 15, OP.logical_shift_right, OP.bitwise_and))
             vop(8, [K("jI"), "EB"], [K("jI")], tt(X("jI"), T.EB[:], X("jI"), OP.subtract))
             vop(8, [K("jI")], [K("eO")], cp(X("eO"), X("jI")))
-            vg(128, et + [K("eO")], [K("eS")], cp(X("eS"), T.E[:, a0:a0 + 2048].indirect(X("eO"))))
+            sg(128, et + [K("eO")], [K("eS")], act(X("eS"), T.E[:, a0:a0 + 2048].indirect(X("eO")), AF.Copy))
             vop(8, [K("nI"), "idx"], [K("nt")], tt(X("nt"), T.idx[:], X("nI"), OP.subtract))
-            vop(8, [K("nt"), "al%d" % h], [K("nt")], tt(X("nt"), X("nt"), T.al[:, 8 * h:8 * h + 8], OP.mult))
+            vop(8, [K("nt"), "al"], [K("nt")], tt(X("nt"), X("nt"), T.al[:, 8 * h:8 * h + 8], OP.mult))
             vop(8, [K("nt"), K("nI")], [K("nS")], tt(X("nS"), X("nI"), X("nt"), OP.add))
-            vg(128, [K("nS"), "LX", "dm"], [K("B")], tt(X("B", 0, 128), X("nS").indirect(T.LX[:]), T.dm[:, 0:128], OP.mult))
-            pop(512, [K("B"), "grpF"], ["P2"], [mm(T.P2[:, 128:256], T.grpF[:], X("B", 0, 128), True, True)])
-            sop(128, [], [K("nBs"), "P2"], act(X("nBs"), T.P2[:, 128:256], AF.Copy))
+            sg(128, [K("S") + "a", "LE"], [K("nBs")], act(X("nBs"), X("S", 0, 128).indirect(T.LE[:, 0:8]), AF.Copy))
+            pop(512, [K("nBs"), "identF"], ["P2"], [mm(T.P2[:, 128:256], X("nBs"), T.identF[:], True, True)])
+            vop(128, [], [K("uA"), "P2"], cp(X("uA"), T.P2[:, 128:256]))
+            vop(128, [K("uA")], [K("uA")], ts(X("uA"), X("uA"), 1023, None, OP.bitwise_and))
             eqt = ["EQ%d%d" % (h, i) for i in range(8)]
-            vg(128, [K("nS"), "LX", K("nBs")], [eqt[7]], tt(X("EQ", 896), X("nS").indirect(T.LX[:]), X("nBs"), OP.is_equal))
+            vg(128, [K("nS"), "LX", K("uA")], [eqt[7]], tt(X("EQ", 896), X("nS").indirect(T.LX[:]), X("uA"), OP.is_equal))
             vop(128, [eqt[7], "ltm"], [eqt[7]], tt(X("EQ", 896), X("EQ", 896), T.ltm[:], OP.mult), 2)
             fs = [mm(T.P3[:, 128:256], T.grp[:], X("EQ", 896), True, False)]
             for c in range(7):
                 s = 16 * (c + 1)
                 e = X("EQ", 128 * c + s, 128 * c + 128)
-                vop(128 - s, [K("nS"), K("nBs")], [eqt[c]], ts(e, X("nBs", s), X("nS", c, c + 1), None, OP.is_equal))
+                vop(128 - s, [K("nS"), K("uA")], [eqt[c]], ts(e, X("uA", s), X("nS", c, c + 1), None, OP.is_equal))
                 fs.append(mm(T.P3[:, 128 + s:256], T.grp[:], e, False, c == 6))
             pop(640, eqt + ["grp"], ["P3"], fs)
-            vop(128, ["dm"], [K("B"), "P3"], tt(X("B", 0, 128), T.P3[:, 128:256], T.dm[:, 0:128], OP.mult))
+            vop(128, ["dmI"], [K("B"), "P3"], tt(X("B", 0, 128), T.P3[:, 128:256], T.dmI[:], OP.mult))
             vop(128, [K("B"), "seg1"], [K("S") + "b"], scan(X("S", 512), T.seg1[:, 0:128], X("B", 0, 128), 0.0, OP.mult, OP.add))
-            vop(8, [K("S") + "b"], [K("nl")], ts(X("nl"), X("S", 527, 640, 16), 0.5, None, OP.is_ge))
-            vop(8, [K("nS"), "idx"], [K("nt")], tt(X("nt"), T.idx[:], X("nS"), OP.subtract))
-            vop(8, [K("nt"), K("nl")], [K("nt")], tt(X("nt"), X("nt"), X("nl"), OP.mult))
-            vop(8, [K("nt"), K("nS")], [K("nl")], tt(X("nl"), X("nS"), X("nt"), OP.add))
+            vop(8, [K("S") + "b", K("nS")], [K("nl")], tt(X("nl"), X("S", 527, 640, 16), X("nS"), OP.max))
+            vop(8, [K("nl"), "idx"], [K("nl")], tt(X("nl"), X("nl"), T.idx[:], OP.min))
             for x in (0, 1):
                 vop(8, [K("nl")], [K("oD%d" % x)], cp(X("oD", x, 16, 2), X("nl")))
             vop(8, [K("nl")], [K("oU")], cp(X("oU"), X("nl")))
-            vg(256, [K("oD0"), K("oD1")] + co_t, [K("T1")], cp(X("T1"), T.coI[:].indirect(X("oD"))))
+            sg(256, [K("oD0"), K("oD1"), "coF0", "coF1", "coF2"], [K("T1")], act(X("T1"), T.coF[:].indirect(X("oD")), AF.Copy))
             vop(256, [K("T1")], [K("T2")], lambda X=X: V.transpose(X("T2"), X("T1")))
             vg(128, [K("T2"), "LP"], [K("fL")], cp(X("fL"), X("T2").indirect(T.LP[:])))
             for k in range(16):
@@ -393,29 +390,26 @@ def rank_program(g, core, T, topo):
             vop(128, ["eS_%d" % h, "oU_%d" % h], x_t, cp(T.Xw[:].indirect(T.oU[:, 8 * h:8 * h + 8]), T.eS[:, 128 * h:128 * h + 128]), SC)
 
         F = lambda src, o, first, last: [mm(T.P4[:, 256:352], T.selX[:, 128 * r:128 * r + 128], src[:, o + r:o + 1536:16], first and r == 0, last and r == 15) for r in range(16)]
-        pop(1536, ["FsB0", "selX"], ["P4"], F(T.FsB0, 0, True, False))
+        pop(1632, ["FsB0", "selX", "Fc", "idBig"], ["P4"], F(T.FsB0, 0, True, False) + [mm(T.P4[:, 256:352], T.idBig[:], T.Fc[:], False, False)])
         for x in (0, 1):
             gop(256, [], ["Vw%d" % x], iof(T["Vw%d" % x][:, 0:256], [[1, 256]], 2560))
         pop(1536, ["FsB1", "selX"], ["P4"], F(T.FsB1, 0, False, False))
         pop(1536, ["Fv", "selX"], ["P4"], F(T.Fv, 1024, False, True))
-        vop(96, [], ["Fn", "P4"], ts(T.Fn[:], T.P4[:, 256:352], 384.0 * 8 ** t, None, OP.is_ge))
-        vop(96, ["Fn", "Fp"], ["Fp"], tt(T.Fp[:], T.Fp[:], T.Fn[:], OP.max), 2)
+        vop(96, [], ["Fp", "P4"], ts(T.Fp[:], T.P4[:, 256:352], 384.0 * 8 ** t, None, OP.is_ge))
         vop(96, ["Fp", "one96"], ["Fi"], scan(T.Fi[:], T.one96[:], T.Fp[:], 0.0, OP.mult, OP.add), 0.5)
-        pop(192, ["Fp", "Fi", "ntri", "grp"], ["P7"], [mm(T.P7[:, 0:96], T.ntri[:], T.Fp[:], True, False), mm(T.P7[:, 0:96], T.grp[:], T.Fi[:], False, True)])
-        vop(96, ["Ld1"], ["s96", "P7"], tt(T.s96[:], T.P7[:, 0:96], T.Ld1[:], OP.subtract))
-        vop(96, [], ["t96", "P7"], ts(T.t96[:], T.P7[:, 0:96], 256.0, None, OP.is_le))
-        vop(96, ["t96", "Fp"], ["t96"], tt(T.t96[:], T.t96[:], T.Fp[:], OP.mult), 2)
-        vop(96, ["t96", "s96"], ["s96"], tt(T.s96[:], T.s96[:], T.t96[:], OP.mult), 2)
-        vop(96, ["s96", "Ld"], ["s96"], tt(T.s96[:], T.s96[:], T.Ld[:], OP.add), 2)
-        vop(96, ["s96"], ["Lv"], cp(T.Lv[:], T.s96[:]))
+        p7 = T.P7[:, 0:96]
+        pop(288, ["Fp", "ident", "c4k", "nid4k", "ntri"], ["P7"], [mm(p7, T.ident[:], T.c4k[:], True, False), mm(p7, T.nid4k[:], T.Fp[:], False, False), mm(p7, T.ntri[:], T.Fp[:], False, False)])
+        pop(96, ["Fi", "grp"], ["P7"], [mm(p7, T.grp[:], T.Fi[:], False, True)])
+        vop(96, ["Ld1"], ["s96", "P7"], tt(T.s96[:], p7, T.Ld1[:], OP.min))
+        vop(96, ["s96"], ["Lv"], ts(T.Lv[:], T.s96[:], -1.0, None, OP.add))
+        vop(96, [], ["t96", "P7"], ts(T.t96[:], p7, 256.0, None, OP.is_le))
         vop(768, ["Lv", "iotaV"], ["Vw0"], cp(T.Vw0[:].indirect(T.Lv[:, 0:48]), T.iotaV[:, 0:768]), SC)
         sop(768, ["Lv", "iotaV"], ["Vw1"], act(T.Vw1[:].indirect(T.Lv[:, 48:96]), T.iotaV[:, 768:1536], AF.Silu), SC)
-        vop(96, ["t96", "Fp"], ["Fp"], tt(T.Fp[:], T.Fp[:], T.t96[:], OP.subtract), 2)
+        vop(96, ["t96", "Fp"], ["Fc"], tt(T.Fc[:], T.Fp[:], T.t96[:], OP.subtract), 2)
         vop(256, ["Vw0", "Vw1"], ["vS"], tt(T.vS[:], T.Vw0[:, 0:256], T.Vw1[:, 0:256], OP.min), 2)
         vop(256, ["vS", "dm"], ["vX"], tt(T.vX[:], T.vS[:], T.dm[:, 0:256], OP.mult), 2)
         vop(256, ["vX", "seg1"], ["vS"], scan(T.vS[:], T.seg1[:], T.vX[:], 0.0, OP.mult, OP.add))
-        vop(16, ["vS"], ["vI"], cp(T.accI[:], T.vS[:, 15::16]))
-        vop(16, ["vI"], ["vL"], cp(T.vL[:], T.accI[:]))
+        vop(16, ["vS"], ["vL"], cp(T.vL[:], T.vS[:, 15::16]))
         vg(256, ["vL"] + su_t, ["sR"], cp(T.sR[:], T.suI[:].indirect(T.vL[:])))
         for q in range(8):
             a, h = 512 * q, q // 4
@@ -433,7 +427,7 @@ def rank_program(g, core, T, topo):
                     tt(T.rs[:, 128 * h:128 * h + 128], T.z[:, b + 15:b + 2048:16], T.az[:, b + 15:b + 2048:16], OP.add), 2)
         vop(256, ["rs0", "rs1"], ["rI"], ts(T.rI[:], T.rs[:], 0.5, -0.25, OP.mult, OP.add))
         vop(256, ["rI", "vL"], x_t, cp(T.Xw[:].indirect(T.vL[:]), T.rI[:]), SC)
-        cur, co_, cur_t = T.land, no, {(h, q): "land%d" % (t + 1) for h in hs for q in (0, 1)}
+        cur, co_, cur_t = T.land, no, ["land%d" % (t + 1)]
     for a in (0, 1280):
         op("Y", 4.0, x_t, [], [lambda a=a: g.sync.dma_start(T.yx[:, a:a + 1280], T.Xw[:, a:a + 1280])], "so", 16, True)
 

from concourse.mybir import AluOpType as OP, AxisListType, ActivationFunctionType as AF

R = 4
SCRATCH = {}
for _n, _w, _t in [
        ("Xw", 2816, "bfloat16"), ("coI", 2560, "int32"), ("coH", 2560, "bfloat16"), ("coF", 2688, "float32"),
        ("suI", 2816, "int32"), ("sh0", 4096, "bfloat16"), ("sh1", 4096, "bfloat16"), ("dls", 1024, "bfloat16"),
        ("M", 4096, "bfloat16"), ("E", 4096, "bfloat16"), ("z", 4096, "bfloat16"), ("az", 4096, "bfloat16"), ("gF", 4096, "bfloat16"),
        ("Fv", 2688, "bfloat16"), ("Fs0", 2688, "float32"), ("Fs1", 2688, "float32"), ("FsB0", 1536, "bfloat16"), ("FsB1", 1536, "bfloat16"),
        ("Vw0", 3072, "float32"), ("Vw1", 3072, "float32"), ("iotaV", 1536, "float32"),
        ("ident", 128, "bfloat16"), ("nident", 128, "bfloat16"), ("nid32", 128, "bfloat16"), ("nid4k", 128, "bfloat16"), ("idBig", 128, "bfloat16"),
        ("c4k", 96, "bfloat16"), ("dmI", 128, "float32"), ("ta", 32, "float32"), ("identF", 128, "float32"), ("grp", 128, "bfloat16"), ("grpF", 128, "float32"),
        ("onesF", 128, "float32"), ("onesB", 128, "bfloat16"), ("ntri", 128, "bfloat16"), ("selX", 2048, "bfloat16"), ("WT", 2048, "bfloat16"),
        ("g8", 8, "float32"), ("g8s", 24, "float32"), ("g8p", 48, "bfloat16"), ("cK", 640, "bfloat16"),
        ("jm", 1024, "float32"), ("segN", 512, "float32"), ("segX", 128, "float32"), ("seg1", 256, "float32"), ("rN", 512, "bfloat16"), ("rX", 512, "bfloat16"),
        ("dm", 640, "float32"), ("ltm", 128, "bfloat16"), ("pI", 8, "int32"), ("pT", 32, "int32"), ("pF", 8, "float32"),
        ("eI", 64, "int32"), ("LE", 40, "uint16"), ("LX", 8, "uint16"), ("LP", 8, "uint16"), ("Ld1", 96, "float32"),
        ("idx", 8, "float32"), ("EB", 8, "float32"), ("one96", 96, "bfloat16"),
        ("stv", 512, "bfloat16"), ("sts", 512, "float32"), ("wt_", 8, "bfloat16"), ("wtF", 8, "float32"), ("thI", 8, "int32"), ("thF", 8, "float32"),
        ("thr", 8, "float32"), ("th16", 8, "float32"), ("gT", 128, "float32"), ("laI", 16, "int32"), ("lbI", 16, "int32"),
        ("abI", 32, "float32"), ("land", 128, "float32"), ("abo", 128, "float32"), ("abU", 32, "uint16"),
        ("al", 16, "float32"), ("acc", 8, "float32"), ("acJ", 16, "int32"),
        ("df", 512, "uint16"), ("dfH", 512, "bfloat16"), ("dfF", 512, "float32"),
        ("Fp", 96, "bfloat16"), ("Fc", 96, "bfloat16"), ("Fi", 96, "bfloat16"), ("t96", 96, "float32"), ("s96", 96, "float32"), ("Lv", 96, "uint16"),
        ("vX", 256, "float32"), ("vS", 256, "float32"), ("vL", 16, "uint16"), ("sR", 256, "uint16"), ("rs", 256, "float32"), ("rI", 256, "int32")]:
    SCRATCH[_n] = ("sbuf", [128, _w], _t)
HALF = {}
for _n, _w, _t in [("S", 640, "float32"), ("B", 640, "float32"), ("dL", 8, "uint16"), ("sT", 128, "uint16"),
                   ("uI", 128, "int32"), ("uA", 128, "int32"), ("uB", 128, "int32"), ("nO", 128, "uint16"), ("nP", 128, "float32"),
                   ("vI", 8, "int32"), ("nI", 8, "int32"), ("jI", 8, "int32"), ("eO", 8, "uint16"), ("nS", 8, "float32"), ("nt", 8, "float32"), ("nl", 8, "float32"),
                   ("nBs", 128, "float32"), ("EQ", 1024, "bfloat16"), ("oU", 8, "uint16"), ("oD", 16, "uint16"), ("T1", 256, "float32"),
                   ("T2", 256, "float32"), ("fL", 128, "uint16"), ("eS", 128, "bfloat16")]:
    SCRATCH[_n] = ("sbuf", [128, 2 * _w], _t)
    HALF[_n] = _w
for _b in range(8):
    SCRATCH["P%d" % _b] = ("psum", [128, 512], "float32")

LOADS = ["la", "lb", "dl", "co0", "co1", "x0", "x1", "su0", "su1", "wt", "th"]
SEMAPHORES = ["sv", "ss", "sp", "sg", "ls", "so"] + ["ld_" + n for n in LOADS] + ["rdl%d" % t for t in (1, 2, 3)] + ["rab%d" % t for t in (1, 2, 3)]

CY, WAKE, LAM, GA, SC = 0.83e-3, 0.1, 0.0, 1.5, 3.5
SPATH = {1: ((1, 3), (1, 2, 3)), 2: ((1, 3), (1, 3))}
MPATH = {1: ((1, 3), (3,)), 2: ((), (3,))}
FLAG_S = (tuple(range(10)), tuple(range(5)))
REN_S = (1, 2, 3, 4, 5, 6, 7)
ORDER = {}


def schedule(ops):
    n = len(ops)
    succ = [[] for _ in ops]
    for i, o in enumerate(ops):
        for d in o["deps"]:
            succ[d].append(i)
    pri = [0.0] * n
    for i in range(n - 1, -1, -1):
        pri[i] = ops[i]["c"] + max([pri[s] + WAKE for s in succ[i]], default=0.0)
    need = [len(o["deps"]) for o in ops]
    early, start, free, out = [0.0] * n, [0.0] * n, {}, []
    ready = {i for i in range(n) if need[i] == 0}
    while ready:
        best = {}
        for i in ready:
            e = ops[i]["e"]
            best[e] = min(best.get(e, 1e18), max(early[i], free.get(e, 0.0)))
        e = min(best, key=lambda q: (best[q], q))
        i = max((j for j in ready if ops[j]["e"] == e and max(early[j], free.get(e, 0.0)) <= best[e] + 0.02), key=lambda j: (pri[j] - LAM * j, -j))
        s = start[i] = max(early[i], free.get(e, 0.0))
        free[e] = s + (0.05 if ops[i]["async"] else ops[i]["c"])
        ready.discard(i)
        out.append(i)
        for j in succ[i]:
            early[j] = max(early[j], s + ops[i]["c"] + WAKE)
            need[j] -= 1
            if need[j] == 0:
                ready.add(j)
    return out, start, max(start[i] + ops[i]["c"] for i in range(n))


def rank_program(g, core, T, topo):
    rank = T.rank_of(core)
    if rank is None:
        return
    N = len(T.cores)
    V, S, PE = g.vector, g.scalar, g.tensor
    ops, lastw, readers = [], {}, {}

    def op(e, c, r, w, fs, sem=None, val=None, isasync=False, order=()):
        i = len(ops)
        deps, soft = {lastw[t] for t in r if t in lastw}, set(order)
        for t in w:
            if t in lastw:
                (soft if t[0] == "P" and ops[lastw[t]]["e"] == e else deps).add(lastw[t])
            deps.update(readers.get(t, ()))
        for t in r:
            readers.setdefault(t, []).append(i)
        for t in w:
            lastw[t] = i
            readers[t] = []
        deps.discard(i)
        ops.append({"e": e, "c": c, "hard": sorted(deps), "deps": sorted(deps | soft), "f": fs, "sem": sem, "val": val, "async": isasync})
        return i

    esem = {"V": "sv", "S": "ss", "PE": "sp", "G": "sg"}
    vop = lambda n, r, w, f, cy=1.0: op("V", 0.055 + max(n * cy, 64) * CY, r, w, [f])
    sop = lambda n, r, w, f, cy=1.0: op("S", 0.07 + max(n * cy, 64) * CY, r, w, [f])
    vg = lambda n, r, w, f: vop(n, r, w, f, GA)
    sg = lambda n, r, w, f: sop(n, r, w, f, GA)
    pop = lambda cyc, r, w, fs: op("PE", cyc * CY, r, w, fs)
    gop = lambda n, r, w, f: op("G", 0.17 + 2 * n * CY, r, w, [f])
    load = lambda q, name, c, w, out, in_: op(q, c, [], w, [lambda: (g.sync if q == "Y" else S).dma_start(out, in_)], "ld_" + name, 16, True)

    def ts(out, a, s1, s2, o0, o1=None):
        return (lambda: V.tensor_scalar(out, a, s1, s2, o0)) if o1 is None else (lambda: V.tensor_scalar(out, a, s1, s2, o0, o1))

    tt = lambda out, a, b, o: (lambda: V.tensor_tensor(out, a, b, o))
    cp = lambda out, a: (lambda: V.tensor_copy(out, a))
    fill = lambda out, c: (lambda: V.memset(out, c))
    act = lambda out, a, f, **k: (lambda: S.activation(out, a, f, **k))
    mm = lambda out, l, r, a, b: (lambda: PE.matmul(out, l, r, a, b))
    scan = lambda out, a, b, i, o0, o1: (lambda: V.tensor_tensor_scan(out, a, b, i, o0, o1))
    iof = lambda out, pat, base: (lambda: g.iota(out, pat, base, 0, allow_small_or_imprecise_dtypes=True))
    ioi = lambda out, pat, base, cm: (lambda: g.iota(out, pat, base, cm))
    sel = lambda out, a, pat, o, base, cm: (lambda: g.affine_select(out, a, pat, o, 0.0, base, cm))
    turn = [0]

    def bank():
        turn[0] += 1
        return 5 + turn[0] % 3

    load("Y", "la", 2, ["laI"], T.laI[:], T.la[:])
    load("Y", "lb", 2, ["lbI"], T.lbI[:], T.lb[:])
    load("S", "dl", 2.5, ["dl0"], T.dls[:, 0:256], T.dl[:])
    load("Y", "co0", 6, ["co0"], T.coI[:, 0:1280], T.co[:, 0:1280])
    load("S", "co1", 6, ["co1"], T.coI[:, 1280:2560], T.co[:, 1280:2560])
    load("Y", "x0", 8, ["X", "Xa"], T.Xw[:, 0:1280], T.x0[:, 0:1280])
    load("S", "x1", 8, ["Xb"], T.Xw[:, 1280:2560], T.x0[:, 1280:2560])
    load("Y", "wt", 3, ["wt"], T.wt_[:, 0:1], T.wt[:])
    load("Y", "th", 3, ["thI"], T.thI[0:8, 0:1], T.th[:])
    load("Y", "su0", 12, ["su0"], T.suI[:, 0:1280], T.su[:, 0:1280])
    load("Y", "su1", 12, ["su1"], T.suI[:, 1280:2560], T.su[:, 1280:2560])
    co_t, su_t, x_t = ["co0", "co1"], ["su0", "su1", "su2"], ["X", "Xa", "Xb"]

    gop(1, [], ["pI"], ioi(T.pI[:, 0:1], [[0, 1]], 0, 1))
    gop(256, [], ["jm"], iof(T.jm[:], [[0, 64], [1, 16]], 0))
    vop(1, ["pI"], ["pT"], ts(T.pT[:, 0:1], T.pI[:, 0:1], 15, None, OP.bitwise_and))
    vop(1, ["pT"], ["pF"], cp(T.pF[:, 0:1], T.pT[:, 0:1]))
    vop(640, ["jm", "pF"], ["dm"], ts(T.dm[:], T.jm[:, 0:640], T.pF[:, 0:1], None, OP.is_equal))
    vop(512, ["jm"], ["segN"], ts(T.segN[:], T.jm[:, 0:512], 0.0, 1e9, OP.is_equal, OP.mult))
    gop(40, [], ["eI"], ioi(T.eI[:, 0:40], [[16, 40]], 15, 0))
    vop(40, ["eI"], ["LE"], cp(T.LE[:], T.eI[:, 0:40]))
    vop(128, [], ["onesB"], fill(T.onesB[:], 1.0))
    vop(128, [], ["onesF"], fill(T.onesF[:], 1.0))
    gop(128, ["onesB"], ["ident"], sel(T.ident[:], T.onesB[:], [[-1, 128]], OP.is_equal, 0, 1))
    for nm, c in (("nident", -1.0), ("nid32", -32.0), ("nid4k", -4096.0), ("idBig", 1048576.0)):
        vop(128, ["ident"], [nm], ts(T[nm][:], T.ident[:], c, None, OP.mult))
    vop(96, [], ["c4k"], fill(T.c4k[:], 4096.0))
    gop(128, [], ["dmI"], iof(T.dmI[:], [[1, 128]], 2560))
    vop(128, ["dmI", "dm"], ["dmI"], tt(T.dmI[:], T.dmI[:], T.dm[:, 0:128], OP.mult), 2)
    gop(8, ["onesF"], ["g8"], sel(T.g8[:], T.onesF[:, 0:8], [[-16, 8]], OP.is_ge, 0, 1))
    gop(8, ["g8"], ["g8"], sel(T.g8[:], T.g8[:], [[16, 8]], OP.is_ge, 15, -1))
    for i, s in enumerate((2048.0, 512.0, 16.0, 2048.0, 512.0, 16384.0)):
        vop(8, ["g8"], ["g8p"], ts(T.g8p[:, 8 * i:8 * i + 8], T.g8[:], s, None, OP.mult))
    for i, s in enumerate((32.0, -4128.0, 1.0)):
        vop(8, ["g8"], ["g8s"], ts(T.g8s[:, 8 * i:8 * i + 8], T.g8[:], s, None, OP.mult))
    for i, (s, v) in enumerate(((128, -160), (32, 5120), (1, 0), (128, -160), (32, 5120))):
        gop(128, [], ["cK"], iof(T.cK[:, 128 * i:128 * i + 128], [[0, 8], [s, 16]], v))
    gop(128, ["onesF"], ["grpF"], sel(T.grpF[:], T.onesF[:], [[-16, 8], [0, 16]], OP.is_ge, 0, 1))
    gop(128, ["grpF"], ["grpF"], sel(T.grpF[:], T.grpF[:], [[16, 8], [0, 16]], OP.is_ge, 15, -1))
    vop(128, ["grpF"], ["grp"], cp(T.grp[:], T.grpF[:]))
    gop(128, ["onesF"], ["gT"], sel(T.gT[:], T.onesF[:], [[1, 8], [0, 16]], OP.is_equal, 0, -1))
    gop(128, ["onesF"], ["identF"], sel(T.identF[:], T.onesF[:], [[-1, 128]], OP.is_equal, 0, 1))
    vop(1, ["thI"], ["thF"], cp(T.thF[0:8, 0:1], T.thI[0:8, 0:1]))
    pop(256, ["gT", "thF"], ["P7"], [mm(T.P7[:, 0:1], T.gT[0:8, :], T.thF[0:8, 0:1], True, True)])
    vop(1, [], ["th16", "P7"], ts(T.th16[:, 0:1], T.P7[:, 0:1], 16.0, None, OP.mult))
    vop(1, ["th16"], ["thr"], cp(T.thr[:, 0:1], T.th16[:, 0:1]))
    for j in range(16):
        gop(128, ["grp"], ["selX"], sel(T.selX[:, 128 * j:128 * j + 128], T.grp[:], [[0, 8], [1, 16]], OP.is_equal, -j, 0))
    vop(1, ["wt"], ["wtF"], cp(T.wtF[:, 0:1], T.wt_[:, 0:1]))
    vop(2048, ["selX", "wtF"], ["WT"], ts(T.WT[:], T.selX[:], T.wtF[:, 0:1], None, OP.mult), 0.5)
    vop(128, ["jm"], ["segX"], ts(T.segX[:], T.jm[:, 0:128], 0.0, 1e9, OP.is_gt, OP.mult))
    vop(256, ["jm"], ["seg1"], ts(T.seg1[:], T.jm[:, 0:256], 0.0, None, OP.is_gt))
    vop(512, ["jm"], ["rN"], ts(T.rN[:], T.jm[:, 0:512], 0.0, 64.0, OP.is_equal, OP.mult))
    vop(512, ["jm"], ["rX"], ts(T.rX[:], T.jm[:, 0:512], 0.0, 64.0, OP.is_gt, OP.mult))
    vop(128, ["jm", "pF"], ["ltm"], ts(T.ltm[:], T.jm[:, 0:128], T.pF[:, 0:1], None, OP.is_gt))
    vop(96, [], ["one96"], fill(T.one96[:], 1.0))
    vop(96, [], ["Fc"], fill(T.Fc[:], 0.0))
    vop(2688, [], ["Fv"], fill(T.Fv[:], 0.0), 0.5)
    for h in (0, 1):
        gop(2688, [], ["Fs%d" % h], iof(T["Fs%d" % h][:], [[0, 2688]], 0))
    vop(256, [], ["su2"], fill(T.suI[:, 2560:2816], 0))
    gop(128, [], ["coF2"], iof(T.coF[:, 2560:2688], [[1, 128]], 2560))
    gop(1536, [], ["iotaV"], iof(T.iotaV[:], [[1, 1536]], 1024))
    sop(1536, ["iotaV"], ["iotaV"], act(T.iotaV[:], T.iotaV[:], AF.Identity, bias=0.25))
    gop(8, [], ["eI2"], ioi(T.eI[:, 48:56], [[1, 8]], 0, 0))
    vop(8, ["eI2"], ["LX"], cp(T.LX[:], T.eI[:, 48:56]))
    gop(8, [], ["idx"], iof(T.idx[:], [[16, 8]], 2560))
    vop(8, ["pF", "idx"], ["idx"], ts(T.idx[:], T.idx[:], T.pF[:, 0:1], None, OP.add))
    gop(96, [], ["Ld1"], iof(T.Ld1[:], [[16, 96]], 1537))
    vop(96, ["pF", "Ld1"], ["Ld1"], ts(T.Ld1[:], T.Ld1[:], T.pF[:, 0:1], None, OP.add))
    vop(1, ["pF"], ["pF2"], ts(T.pF[:, 1:2], T.pF[:, 0:1], 16.0, None, OP.mult))
    vop(1, ["pF"], ["pFn"], ts(T.pF[:, 6:7], T.pF[:, 0:1], -1024.0, 15360.0, OP.mult, OP.add))
    gop(8, [], ["EB"], iof(T.EB[:], [[256, 8]], 15))
    vop(8, ["pF2", "EB"], ["EB"], ts(T.EB[:], T.EB[:], T.pF[:, 1:2], None, OP.add))
    vop(1, ["pI"], ["pT1"], ts(T.pT[:, 8:9], T.pI[:, 0:1], 7, None, OP.bitwise_and))
    vop(1, ["pI"], ["pT2"], ts(T.pT[:, 16:17], T.pI[:, 0:1], 16, None, OP.bitwise_and))
    vop(1, ["pI"], ["pT3"], ts(T.pT[:, 24:25], T.pI[:, 0:1], 3, 1, OP.logical_shift_right, OP.bitwise_and))
    vop(1, ["pT2"], ["pF3"], cp(T.pF[:, 3:4], T.pT[:, 16:17]))
    vop(1, ["pT1", "pF3"], ["pF4"], ts(T.pF[:, 4:5], T.pT[:, 8:9], 32.0, T.pF[:, 3:4], OP.mult, OP.add))
    vop(1, ["pT3", "pF4"], ["pF5"], tt(T.pF[:, 5:6], T.pT[:, 24:25], T.pF[:, 4:5], OP.add))
    gop(8, [], ["eI3"], ioi(T.eI[:, 56:64], [[2, 8]], 0, 0))
    vop(8, ["eI3", "pF5"], ["LP"], ts(T.LP[:], T.eI[:, 56:64], T.pF[:, 5:6], None, OP.add))
    gop(128, ["onesB"], ["ntri"], sel(T.ntri[:], T.onesB[:], [[-1, 128]], OP.is_gt, 0, 1))
    vop(128, ["ntri", "grp"], ["ntri"], tt(T.ntri[:], T.ntri[:], T.grp[:], OP.mult))
    vop(128, ["ntri"], ["ntri"], ts(T.ntri[:], T.ntri[:], -1.0, None, OP.mult))
    for t in range(R):
        vop(128, [], ["stv%d" % t], fill(T.stv[:, 128 * t:128 * t + 128], float(32 * 8 ** t)))
        vop(128, [], ["sts%d" % t], fill(T.sts[:, 128 * t:128 * t + 128], float(32 * 8 ** t)))
    for x in (0, 1):
        vop(1280, ["co%d" % x], ["coF%d" % x], cp(T.coF[:, 1280 * x:1280 * x + 1280], T.coI[:, 1280 * x:1280 * x + 1280]))
        sop(1280, ["coF%d" % x], ["coH%d" % x], act(T.coH[:, 1280 * x:1280 * x + 1280], T.coF[:, 1280 * x:1280 * x + 1280], AF.Identity, scale=0.03125, bias=159.515625))

    def send(dst_rank, out, in_, sem, r):
        dst = T.cores[dst_rank]
        rid, pid, _ = topo.addr(dst)
        m = sum(1 << e for e in topo.engines(core, dst)[:4])
        return op("G", 0.6, r, [], [lambda: g.remote_dma(out, in_, T.sem[sem], T.sem.ls, pid, rid, m)], "none", 0)

    for t in (1, 2, 3):
        i = send((rank + t) % N, T.dls[:, 256 * t:256 * t + 256], T.dls[:, 0:256], "rdl%d" % t, ["dl0"])
        op("R", 4.0, [], ["dl%d" % t], [], "rdl%d" % t, 4, True, order=[i])
    for k in range(16):
        if k % 2:
            vop(256, ["dl0"], ["sh0_%d" % k], cp(T.sh0[:, k::16], T.dls[:, 0:256]), 0.5)
        else:
            sop(256, ["dl0"], ["sh0_%d" % k], act(T.sh0[:, k::16], T.dls[:, 0:256], AF.Copy))
    hs = (0, 1)
    for q, nm in enumerate(("laI", "lbI")):
        vop(16, [nm], ["abI%d" % q], cp(T.abI[:, 16 * q:16 * q + 16], T[nm][:]))
    cur, co_, cur_t = T.abI, 0, ["abI0", "abI1"]

    for t in range(R):
        sh = T.sh0 if t % 2 == 0 else T.sh1
        sht = ["sh%d_%d" % (t % 2, k) for k in range(16)]
        if t:
            for k in range(16):
                gop(256, ["dl%d" % t], [sht[k]], sel(sh[:, k::16], T.dls[:, 256 * t:256 * t + 256], [[0, 256]], OP.is_ge, 1, 0))
        no = 32 * t
        vop(32, cur_t, ["abU"], cp(T.abU[:], cur[:, co_:co_ + 32]))
        vg(512, ["abU"] + co_t, ["df"], cp(T.df[:], T.coI[:].indirect(T.abU[:])))
        for nm in ("H", "F"):
            sg(512, ["abU", "co%s0" % nm, "co%s1" % nm], ["df" + nm], act(T["df" + nm][:], T["co" + nm][:, 0:2560].indirect(T.abU[:]), AF.Copy))

        def second(step, h, q, lists, lo, Mb, mt, lt):
            a, zt = 2048 * h + 512 * q, "z%d%d" % (h, q)
            win = T.Xw[:, 0:2560].indirect(lists[:, lo + 32 * q:lo + 32 * q + 32])
            if q in SPATH[step][h]:
                gt, P = "gF%d%d" % (h, q), "P%d" % bank()
                sg(512, x_t + [lt], [gt], act(T.gF[:, a:a + 512], win, AF.Copy))
                pop(1024, ["ident", "nident", gt, mt], [P], [mm(T[P][:], T.nident[:], Mb[:, a:a + 512], True, False), mm(T[P][:], T.ident[:], T.gF[:, a:a + 512], False, True)])
                sop(512, [], [P, "a" + zt], act(T.az[:, a:a + 512], T[P][:], AF.Abs))
            else:
                vg(512, x_t + [lt, mt], [zt], tt(T.z[:, a:a + 512], win, Mb[:, a:a + 512], OP.subtract))
                sop(512, [zt], ["a" + zt], act(T.az[:, a:a + 512], T.z[:, a:a + 512], AF.Abs))

        def moved(step, h, q, lists, lo, lt, Mb, mt):
            a = 2048 * h + 512 * q
            win = T.Xw[:, 0:2560].indirect(lists[:, lo + 32 * q:lo + 32 * q + 32])
            if q in MPATH[step][h]:
                gt, P = "gF%d%d" % (h, q), "P%d" % bank()
                sg(512, x_t + [lt], [gt], act(T.gF[:, a:a + 512], win, AF.Copy))
                pop(1024, ["ident", gt] + sht, [P], [mm(T[P][:], T.ident[:], sh[:, a:a + 512], True, False), mm(T[P][:], T.ident[:], T.gF[:, a:a + 512], False, True)])
                vop(512, [], [P, mt], ts(Mb[:, a:a + 512], T[P][:], 0.0, 63.0, OP.max, OP.min))
                return
            vg(512, x_t + [lt] + sht, [mt], tt(Mb[:, a:a + 512], win, sh[:, a:a + 512], OP.add))
            vop(512, [mt], [mt], ts(Mb[:, a:a + 512], Mb[:, a:a + 512], 0.0, 63.0, OP.max, OP.min), 0.5)

        for h in hs:
            X = lambda n, a=0, b=None, s=1, h=h: T[n][:, h * HALF[n] + a:h * HALF[n] + (HALF[n] if b is None else b):s]
            K = lambda n, h=h: "%s_%d" % (n, h)
            b, a0 = 128 * h, 2048 * h
            for q in range(4):
                moved(1, h, q, T.df, b, "df", T.M, "M%d%d" % (h, q))
            for q in range(4):
                second(1, h, q, T.df, b + 256, T.M, "M%d%d" % (h, q), "df")
            azt = ["az%d%d" % (h, q) for q in range(4)]
            for P, w, c0, d in (("P0", 384, 0, b), ("P1", 256, 384, b + 256)):
                lh, lf = T.dfH[:, d:d + 128], T.dfF[:, d:d + 128]
                pop(w + 768, ["ident", "identF", "nid32", "cK", "dfH", "dfF"], [P], [
                    mm(T[P][:, 0:w], T.ident[:], T.cK[:, c0:c0 + w], True, False), mm(T[P][:, 0:128], lh, T.ident[:], False, False),
                    mm(T[P][:, 128:256], lf, T.identF[:], False, False), mm(T[P][:, 128:256], lh, T.nid32[:], False, False)])
            l = [T.az[:, a0 + k:a0 + 2048:16] for k in range(16)]
            pop(1024, azt + ["g8p"], ["P0"], [mm(T.P0[:, k:384:16], l[k], T.g8p[:, 0:24], False, k == 15) for k in range(16)])
            pop(1024, azt + ["g8p"], ["P1"], [mm(T.P1[:, k:256:16], l[k], T.g8p[:, 24:40], False, k == 15) for k in range(16)])
            vop(384, ["segN"], [K("S") + "a", "P0"], scan(X("S", 0, 384), T.segN[:, 0:384], T.P0[:, 0:384], 1e9, OP.max, OP.min))
            vg(384, [K("S") + "a", "LE", "dm"], [K("B")], tt(X("B", 0, 384), X("S", 0, 384).indirect(T.LE[:, 0:24]), T.dm[:, 0:384], OP.mult))
            vop(256, ["segN"], [K("S") + "b", "P1"], scan(X("S", 384), T.segN[:, 0:256], T.P1[:, 0:256], 1e9, OP.max, OP.min))
            vg(256, [K("S") + "b", "LE", "dm"], [K("B") + "b"], tt(X("B", 384), X("S", 384).indirect(T.LE[:, 0:16]), T.dm[:, 0:256], OP.mult))
            c32, c41, c1 = T.g8s[:, 0:8], T.g8s[:, 8:16], T.g8s[:, 16:24]
            blk = [X("B", 128 * i, 128 * i + 128) for i in range(5)]
            pd, pf, pk = T.P2[:, 8 * h:8 * h + 8], T.P3[:, 8 * h:8 * h + 8], T.P3[:, 16 + 8 * h:24 + 8 * h]
            pop(768, [K("B"), "g8s"], ["P2"], [mm(pd, blk[0], c32, True, False), mm(pd, blk[2], c41, False, False), mm(pd, blk[1], c1, False, True)])
            pop(1024, [K("B"), K("B") + "b", "g8s"], ["P3"], [mm(pf, blk[3], c32, True, False), mm(pf, blk[2], c41, False, False), mm(pf, blk[4], c1, False, True), mm(pk, blk[2], c1, True, True)])
            vop(8, [], [K("dL"), "P2"], cp(X("dL"), pd))
        vop(16, ["thr"], ["al", "P3"], ts(T.al[:], T.P3[:, 16:32], T.thr[:, 0:1], None, OP.is_lt))
        for q, P in ((0, "P2"), (1, "P3")):
            tq = T.ta[:, 16 * q:16 * q + 16]
            vop(16, cur_t, ["ta%d" % q, P], tt(tq, T[P][:, 0:16], cur[:, co_ + 16 * q:co_ + 16 * q + 16], OP.subtract))
            vop(16, ["ta%d" % q, "al"], ["ta%d" % q], tt(tq, tq, T.al[:], OP.mult))
        vop(32, ["ta0", "ta1"] + cur_t, ["abo%d" % t], tt(T.abo[:, no:no + 32], T.ta[:], cur[:, co_:co_ + 32], OP.add))
        if t < R - 1:
            i = send((rank + 1) % N, T.land[:, no:no + 32], T.abo[:, no:no + 32], "rab%d" % (t + 1), ["abo%d" % t])
            op("R", 4.0, [], ["land%d" % (t + 1)], [], "rab%d" % (t + 1), 4, True, order=[i])
            vop(16, ["al"], ["acc"], lambda: V.tensor_reduce(T.acc[:, 0:1], T.al[:], AxisListType.X, OP.add))
            pop(256, ["acc", "onesF"], ["P3"], [mm(T.P3[:, 32:33], T.onesF[:], T.acc[:, 0:1], True, True)])
            vop(1, [], ["acI", "P3"], ts(T.acJ[:, 0:1], T.P3[:, 32:33], -1.0, 2048.0, OP.mult, OP.add))
            vop(1, ["acI"], ["acJ"], ts(T.acJ[:, 8:9], T.acJ[:, 0:1], 63, None, OP.bitwise_and))
            vop(1, ["acJ", "th16"], ["thr"], ts(T.thr[:, 0:1], T.acJ[:, 8:9], 16.0, T.th16[:, 0:1], OP.mult, OP.add))
        else:
            for q, y in enumerate((T.ya, T.yb)):
                u = no + 16 * q
                op("Y", 2.0, ["abo%d" % t], [], [lambda y=y, u=u: g.sync.dma_start(y[:], T.abo[:, u:u + 16])], "so", 16, True)

        for h in hs:
            X = lambda n, a=0, b=None, s=1, h=h: T[n][:, h * HALF[n] + a:h * HALF[n] + (HALF[n] if b is None else b):s]
            K = lambda n, h=h: "%s_%d" % (n, h)
            a0 = 2048 * h
            vg(128, [K("dL")] + su_t[:2], [K("sT")], cp(X("sT"), T.suI[:, 0:2560].indirect(X("dL"))))
            for q in range(4):
                moved(2, h, q, T.sT, 128 * h, K("sT"), T.E, "E%d%d" % (h, q))
            et, azt = ["E%d%d" % (h, q) for q in range(4)], ["az%d%d" % (h, q) for q in range(4)]
            for x in (0, 1):
                pop(1024, et[2 * x:2 * x + 2] + ["WT"], ["P4"], [mm(T.P4[:, 64 * x:64 * x + 64], T.WT[:, 128 * j:128 * j + 128], T.E[:, a0 + 1024 * x + j:a0 + 1024 * x + 1024:16], j == 0, j == 15) for j in range(16)])
            vop(128, [], [K("uI"), "P4"], cp(X("uI"), T.P4[:, 0:128]))
            vop(128, [K("uI")], [K("uI")], ts(X("uI"), X("uI"), 4095, None, OP.bitwise_and))
            vop(128, [K("uI")], [K("uA")], ts(X("uA"), X("uI"), -2048.0, None, OP.add))
            vop(128, [K("uI")], [K("uB")], ts(X("uB"), X("uI"), 3232.0, None, OP.add))
            vop(128, [K("uA"), K("uB")], [K("uA")], tt(X("uA"), X("uA"), X("uB"), OP.mult), 2)
            vop(128, [K("uA")], [K("uI")], ts(X("uI"), X("uA"), 5, 1023, OP.arith_shift_right, OP.bitwise_and))
            vop(128, [K("uI")], [K("nO")], cp(X("nO"), X("uI")))
            vop(128, [K("uI"), "pFn"], [K("nP")], ts(X("nP"), X("uI"), T.pF[:, 6:7], None, OP.add))
            for q in range(4):
                second(2, h, q, T.nO, 128 * h, T.E, "E%d%d" % (h, q), K("nO"))
            pop(512, [K("nP"), "identF"], ["P1"], [mm(T.P1[:, 256:384], X("nP"), T.identF[:], True, False)])
            pop(1024, azt + ["g8p"], ["P1"], [mm(T.P1[:, 256 + j:384:16], T.az[:, a0 + j:a0 + 2048:16], T.g8p[:, 40:48], False, j == 15) for j in range(16)])
            vop(128, ["segX"], [K("S") + "a", "P1"], scan(X("S", 0, 128), T.segX[:], T.P1[:, 256:384], 0.0, OP.min, OP.max))
            vg(128, [K("S") + "a", "LE", "dm"], [K("B")], tt(X("B", 0, 128), X("S", 0, 128).indirect(T.LE[:, 0:8]), T.dm[:, 0:128], OP.mult))
            pop(256, [K("B"), "g8"], ["P2"], [mm(T.P2[:, 16:24], X("B", 0, 128), T.g8[:], True, True)])
            vop(8, [], [K("vI"), "P2"], cp(X("vI"), T.P2[:, 16:24]))
            vop(8, [K("vI")], [K("nI")], ts(X("nI"), X("vI"), 1023, None, OP.bitwise_and))
            vop(8, [K("vI")], [K("jI")], ts(X("jI"), X("vI"), 10, 15, OP.logical_shift_right, OP.bitwise_and))
            vop(8, [K("jI"), "EB"], [K("jI")], tt(X("jI"), T.EB[:], X("jI"), OP.subtract))
            vop(8, [K("jI")], [K("eO")], cp(X("eO"), X("jI")))
            sg(128, et + [K("eO")], [K("eS")], act(X("eS"), T.E[:, a0:a0 + 2048].indirect(X("eO")), AF.Copy))
            vop(8, [K("nI"), "idx"], [K("nt")], tt(X("nt"), T.idx[:], X("nI"), OP.subtract))
            vop(8, [K("nt"), "al"], [K("nt")], tt(X("nt"), X("nt"), T.al[:, 8 * h:8 * h + 8], OP.mult))
            vop(8, [K("nt"), K("nI")], [K("nS")], tt(X("nS"), X("nI"), X("nt"), OP.add))
            sg(128, [K("S") + "a", "LE"], [K("nBs")], act(X("nBs"), X("S", 0, 128).indirect(T.LE[:, 0:8]), AF.Copy))
            pop(512, [K("nBs"), "identF"], ["P2"], [mm(T.P2[:, 128:256], X("nBs"), T.identF[:], True, True)])
            vop(128, [], [K("uA"), "P2"], cp(X("uA"), T.P2[:, 128:256]))
            vop(128, [K("uA")], [K("uA")], ts(X("uA"), X("uA"), 1023, None, OP.bitwise_and))
            eqt = ["EQ%d%d" % (h, i) for i in range(8)]
            vg(128, [K("nS"), "LX", K("uA")], [eqt[7]], tt(X("EQ", 896), X("nS").indirect(T.LX[:]), X("uA"), OP.is_equal))
            vop(128, [eqt[7], "ltm"], [eqt[7]], tt(X("EQ", 896), X("EQ", 896), T.ltm[:], OP.mult), 2)
            fs = [mm(T.P3[:, 128:256], T.grp[:], X("EQ", 896), True, False)]
            for c in range(7):
                s = 16 * (c + 1)
                e = X("EQ", 128 * c + s, 128 * c + 128)
                vop(128 - s, [K("nS"), K("uA")], [eqt[c]], ts(e, X("uA", s), X("nS", c, c + 1), None, OP.is_equal))
                fs.append(mm(T.P3[:, 128 + s:256], T.grp[:], e, False, c == 6))
            pop(640, eqt + ["grp"], ["P3"], fs)
            vop(128, ["dmI"], [K("B"), "P3"], tt(X("B", 0, 128), T.P3[:, 128:256], T.dmI[:], OP.mult))
            vop(128, [K("B"), "seg1"], [K("S") + "b"], scan(X("S", 512), T.seg1[:, 0:128], X("B", 0, 128), 0.0, OP.mult, OP.add))
            vop(8, [K("S") + "b", K("nS")], [K("nl")], tt(X("nl"), X("S", 527, 640, 16), X("nS"), OP.max))
            vop(8, [K("nl"), "idx"], [K("nl")], tt(X("nl"), X("nl"), T.idx[:], OP.min))
            for x in (0, 1):
                vop(8, [K("nl")], [K("oD%d" % x)], cp(X("oD", x, 16, 2), X("nl")))
            vop(8, [K("nl")], [K("oU")], cp(X("oU"), X("nl")))
            sg(256, [K("oD0"), K("oD1"), "coF0", "coF1", "coF2"], [K("T1")], act(X("T1"), T.coF[:].indirect(X("oD")), AF.Copy))
            vop(256, [K("T1")], [K("T2")], lambda X=X: V.transpose(X("T2"), X("T1")))
            vg(128, [K("T2"), "LP"], [K("fL")], cp(X("fL"), X("T2").indirect(T.LP[:])))
            for k in range(16):
                off = X("fL", 8 * k, 8 * k + 8)
                if k in FLAG_S[h]:
                    sop(128, [K("fL"), "sts%d" % t], ["Fs%d" % h], act(T["Fs%d" % h][:].indirect(off), T.sts[:, 128 * t:128 * t + 128], AF.Silu), SC)
                else:
                    vop(128, [K("fL"), "stv%d" % t], ["Fv"], cp(T.Fv[:].indirect(off), T.stv[:, 128 * t:128 * t + 128]), SC)
            sop(1536, ["Fs%d" % h], ["FsB%d" % h], act(T["FsB%d" % h][:], T["Fs%d" % h][:, 1024:2560], AF.Copy))
        for h in (1, 0):
            vop(128, ["eS_%d" % h, "oU_%d" % h], x_t, cp(T.Xw[:].indirect(T.oU[:, 8 * h:8 * h + 8]), T.eS[:, 128 * h:128 * h + 128]), SC)

        F = lambda src, o, first, last: [mm(T.P4[:, 256:352], T.selX[:, 128 * r:128 * r + 128], src[:, o + r:o + 1536:16], first and r == 0, last and r == 15) for r in range(16)]
        pop(1632, ["FsB0", "selX", "Fc", "idBig"], ["P4"], F(T.FsB0, 0, True, False) + [mm(T.P4[:, 256:352], T.idBig[:], T.Fc[:], False, False)])
        for x in (0, 1):
            gop(256, [], ["Vw%d" % x], iof(T["Vw%d" % x][:, 0:256], [[1, 256]], 2560))
        pop(1536, ["FsB1", "selX"], ["P4"], F(T.FsB1, 0, False, False))
        pop(1536, ["Fv", "selX"], ["P4"], F(T.Fv, 1024, False, True))
        vop(96, [], ["Fp", "P4"], ts(T.Fp[:], T.P4[:, 256:352], 384.0 * 8 ** t, None, OP.is_ge))
        vop(96, ["Fp", "one96"], ["Fi"], scan(T.Fi[:], T.one96[:], T.Fp[:], 0.0, OP.mult, OP.add), 0.5)
        p7 = T.P7[:, 0:96]
        pop(288, ["Fp", "ident", "c4k", "nid4k", "ntri"], ["P7"], [mm(p7, T.ident[:], T.c4k[:], True, False), mm(p7, T.nid4k[:], T.Fp[:], False, False), mm(p7, T.ntri[:], T.Fp[:], False, False)])
        pop(96, ["Fi", "grp"], ["P7"], [mm(p7, T.grp[:], T.Fi[:], False, True)])
        vop(96, ["Ld1"], ["s96", "P7"], tt(T.s96[:], p7, T.Ld1[:], OP.min))
        vop(96, ["s96"], ["Lv"], ts(T.Lv[:], T.s96[:], -1.0, None, OP.add))
        vop(96, [], ["t96", "P7"], ts(T.t96[:], p7, 256.0, None, OP.is_le))
        vop(768, ["Lv", "iotaV"], ["Vw0"], cp(T.Vw0[:].indirect(T.Lv[:, 0:48]), T.iotaV[:, 0:768]), SC)
        sop(768, ["Lv", "iotaV"], ["Vw1"], act(T.Vw1[:].indirect(T.Lv[:, 48:96]), T.iotaV[:, 768:1536], AF.Silu), SC)
        vop(96, ["t96", "Fp"], ["Fc"], tt(T.Fc[:], T.Fp[:], T.t96[:], OP.subtract), 2)
        vop(256, ["Vw0", "Vw1"], ["vS"], tt(T.vS[:], T.Vw0[:, 0:256], T.Vw1[:, 0:256], OP.min), 2)
        vop(256, ["vS", "dm"], ["vX"], tt(T.vX[:], T.vS[:], T.dm[:, 0:256], OP.mult), 2)
        vop(256, ["vX", "seg1"], ["vS"], scan(T.vS[:], T.seg1[:], T.vX[:], 0.0, OP.mult, OP.add))
        vop(16, ["vS"], ["vL"], cp(T.vL[:], T.vS[:, 15::16]))
        vg(256, ["vL"] + su_t, ["sR"], cp(T.sR[:], T.suI[:].indirect(T.vL[:])))
        for q in range(8):
            a, h = 512 * q, q // 4
            gt, zt, at = "gF%d%d" % (h, q % 4), "z%d%d" % (h, q % 4), "az%d%d" % (h, q % 4)
            win = T.Xw[:, 0:2560].indirect(T.sR[:, 32 * q:32 * q + 32])
            if q in REN_S:
                sg(512, x_t + ["sR"], [gt], act(T.gF[:, a:a + 512], win, AF.Copy))
            else:
                vg(512, x_t + ["sR"], [gt], cp(T.gF[:, a:a + 512], win))
            vop(512, [gt, "rX"], [zt], scan(T.z[:, a:a + 512], T.rX[:], T.gF[:, a:a + 512], 0.0, OP.min, OP.max), 0.5)
            vop(512, [gt, "rN"], [at], scan(T.az[:, a:a + 512], T.rN[:], T.gF[:, a:a + 512], 64.0, OP.max, OP.min), 0.5)
            if q % 4 == 3:
                b = 2048 * h
                vop(128, [x + "%d%d" % (h, i) for i in range(4) for x in ("z", "az")], ["rs%d" % h],
                    tt(T.rs[:, 128 * h:128 * h + 128], T.z[:, b + 15:b + 2048:16], T.az[:, b + 15:b + 2048:16], OP.add), 2)
        vop(256, ["rs0", "rs1"], ["rI"], ts(T.rI[:], T.rs[:], 0.5, -0.25, OP.mult, OP.add))
        vop(256, ["rI", "vL"], x_t, cp(T.Xw[:].indirect(T.vL[:]), T.rI[:]), SC)
        cur, co_, cur_t = T.land, no, ["land%d" % (t + 1)]
    for a in (0, 1280):
        op("Y", 4.0, x_t, [], [lambda a=a: g.sync.dma_start(T.yx[:, a:a + 1280], T.Xw[:, a:a + 1280])], "so", 16, True)

    if "o" not in ORDER:
        ORDER["o"], ORDER["start"], ORDER["end"] = schedule(ops)
        ORDER["ops"] = [(o["e"], o["c"]) for o in ops]
    queue = {"V": V, "S": S, "PE": PE, "G": g, "Y": g.sync}
    count, known = {}, {q: {} for q in queue}
    for i in ORDER["o"]:
        o = ops[i]
        e, clk = o["e"], {}
        if e != "R":
            kn = known[e]
            for d in reversed(o["hard"]):
                x = ops[d]
                if x["sem"] != "none" and kn.get(x["s"], 0) < x["n"]:
                    queue[e].wait_ge(T.sem[x["s"]], x["n"])
                    for s, v in x["clk"].items():
                        kn[s] = max(kn.get(s, 0), v)
            clk = dict(kn)
        s = o["sem"] or esem[e]
        inc = 16 if o["sem"] else 1
        for f in o["f"]:
            ins = f()
            if s != "none":
                ins.then_inc(T.sem[s], inc)
                count[s] = count.get(s, 0) + inc
        if e == "R":
            count[s] = o["val"]
        if s != "none":
            o["s"], o["n"] = s, count[s]
            clk[s] = count[s]
        o["clk"] = clk
    for s in SEMAPHORES:
        if count.get(s, 0) > known["Y"].get(s, 0):
            g.sync.wait_ge(T.sem[s], count[s])
    g.wait_ge(T.sem.ls, 4 * 6)
